import numpy as np
import ml_dtypes


def mxq(x, axis, fmt="e4m3"):
    dtype, down = {"e4m3": (ml_dtypes.float8_e4m3fn, 7), "e5m2": (ml_dtypes.float8_e5m2, 14)}[fmt]
    v = np.moveaxis(np.asarray(x, np.float32).astype(ml_dtypes.bfloat16).astype(np.float64), axis, -1)
    blocks = v.reshape(v.shape[:-1] + (-1, 32))
    amax = np.abs(blocks).max(-1, keepdims=True)
    byte = np.maximum(np.where(amax > 0, np.frexp(amax)[1] - 1 + 127, 0) - down, 1)
    scale = np.exp2(byte - 127.0)
    codes = (blocks / scale).astype(np.float32).astype(dtype).astype(np.float64)
    return np.moveaxis((codes * scale).reshape(v.shape), -1, axis)


WIDE = False


def mx_kscale(k):
    if not WIDE:
        return np.ones(k)
    levels = np.array([10, -10, 5, -5, 0])
    if k % 512:
        return np.exp2(np.random.permutation(np.resize(levels, k // 32))).repeat(32)
    a = np.empty((k // 512, 16))
    for p in range(k // 512):
        a[p, :8] = np.random.permutation(np.resize(levels, 8))
        for g in range(8):
            far = levels[np.abs(levels - a[p, g]) >= 10]
            a[p, g + 8] = far[np.random.randint(len(far))]
    return np.exp2(a.ravel()).repeat(32)


BF16 = ml_dtypes.bfloat16


def bf(x):
    return np.asarray(x, np.float32).astype(BF16)


def f64(x):
    return np.asarray(x).astype(np.float64)


E2M1 = np.array([0.0, 0.5, 1.0, 1.5, 2.0, 3.0, 4.0, 6.0, -0.0, -0.5, -1.0, -1.5, -2.0, -3.0, -4.0, -6.0])


def pack_weight(w, fmt):
    k, n = w.shape
    w = f64(bf(w)).reshape(k // 32, 32, n)
    amax = np.abs(w).max(1)
    if fmt == "e4m3":
        byte = np.frexp(amax)[1] - 1 + 127 - 7
    else:
        mant, ex = np.frexp(amax / 6.0)
        byte = np.where(mant > 0.5, ex, ex - 1) + 127
    byte = np.clip(np.where(amax > 0, byte, 1), 1, 254)
    scaled = (w * np.exp2(127.0 - byte)[:, None, :]).reshape(k, n).astype(np.float32)
    by_word = np.ascontiguousarray(scaled.reshape(k // 512, 128, 4, n).transpose(0, 1, 3, 2))
    if fmt == "e4m3":
        words = by_word.astype(ml_dtypes.float8_e4m3fn).view(np.uint8)
    else:
        c = by_word.astype(ml_dtypes.float4_e2m1fn).view(np.uint8) & 0xF
        words = c[..., 0::2] | (c[..., 1::2] << 4)
    return np.ascontiguousarray(words), np.ascontiguousarray(byte.astype(np.uint8).reshape(k // 512, 16, n))


def unpack_weight(words, scales, fmt):
    g, p, n, _ = words.shape
    if fmt == "e4m3":
        vals = np.ascontiguousarray(words).view(ml_dtypes.float8_e4m3fn).astype(np.float64)
    else:
        nib = np.empty((g, p, n, 4), np.uint8)
        nib[..., 0::2] = words & 0xF
        nib[..., 1::2] = words >> 4
        vals = E2M1[nib]
    vals = vals * np.repeat(np.exp2(scales.astype(np.float64) - 127.0), 8, axis=1)[..., None]
    return vals.transpose(0, 1, 3, 2).reshape(g * 512, n)
def pack4(w):
    words, scales = pack_weight(w, "e2m1")
    return words.reshape(words.shape[0], 128, -1), scales


def unpack4(words, scales):
    return unpack_weight(words.reshape(words.shape[0], 128, -1, 2), scales, "e2m1")


def planes(Y):
    n, m = Y.shape
    b = f64(bf(Y)).reshape(n // 32, 32, m)
    amax = np.abs(b).max(1)
    byte = np.clip(np.where(amax > 0, np.frexp(amax)[1] - 1 + 127 - 7, 1), 1, 254)
    codes = (b * np.exp2(127.0 - byte)[:, None, :]).reshape(n, m).astype(np.float32).astype(ml_dtypes.float8_e4m3fn).view(np.uint8)
    words = codes.reshape(n // 512, 128, 4, m).transpose(0, 1, 3, 2)
    return np.ascontiguousarray(words), np.ascontiguousarray(byte.astype(np.uint8).reshape(n // 512, 16, m))


UNITS, VARS, OUTS = 1024, 1024, 1536

def setup_inputs():
    eye = np.eye(VARS)
    s = mx_kscale(VARS)
    b = 0.35 * np.random.randn(VARS, VARS) / np.sqrt(VARS) * (1.0 - eye)
    b_words, b_scales = pack4(b * s[None, :] / s[:, None])
    b = unpack4(b_words, b_scales) * s[:, None] / s[None, :]
    strength = np.random.uniform(0.5, 1.5, VARS)
    r = np.linalg.inv(eye - b * strength[None, :]) - eye
    x = np.linalg.solve((eye - b).T, np.random.randn(VARS, UNITS)).T
    shift = 0.5 * np.random.randn(VARS)
    spread = np.exp(0.8 * np.random.randn(OUTS))
    c = np.random.randn(VARS, OUTS) / np.sqrt(VARS) * spread[None, :]
    bias = 0.4 * np.random.randn(OUTS) * spread
    return {"x": bf(x * s[None, :]), "b_words": b_words, "b_scales": b_scales,
            "shift": bf(shift * s), "r": bf(r * s[None, :] / s[:, None]),
            "c": bf(c / s[:, None]), "bias": bf(bias)}

def reference(x, b_words, b_scales, shift, r, c, bias):
    x, shift, r, c, bias = f64(x), f64(shift), f64(r), f64(c), f64(bias)
    b = unpack4(b_words, b_scales)
    e = x - (mxq(x, 1, "e4m3") @ b) + shift
    z = e + (mxq(e, 1, "e4m3") @ mxq(r, 0, "e4m3"))
    y = (mxq(z, 1, "e4m3") @ mxq(c, 0, "e4m3")) + bias
    Y = y.T
    words, scales = planes(Y)
    return y, words, scales

@@ -1,0 +1,469 @@
+from contextlib import ExitStack
+
+import concourse.mybir as mybir
+from concourse.masks import make_identity
+
+UNITS, VARS, OUTS = 1024, 1024, 1536
+FLOPS = 2 * UNITS * VARS * (2 * VARS + OUTS)
+
+F32 = mybir.dt.float32
+BF16 = mybir.dt.bfloat16
+U32 = mybir.dt.uint32
+I32 = mybir.dt.int32
+U8 = mybir.dt.uint8
+FP8X4 = mybir.dt.float8_e4m3fn_x4
+FP4X4 = mybir.dt.float4_e2m1fn_x4
+ADD = mybir.AluOpType.add
+SUB = mybir.AluOpType.subtract
+MULT = mybir.AluOpType.mult
+
+P = 128
+PACK = 4
+GROUP = P * PACK
+VG = VARS // GROUP
+OG = OUTS // GROUP
+UT = UNITS // P
+HALF = 512
+PIECE = 256
+
+
+def tile_structural_model_counterfactual_k1_kernel(
+    tc, x, b_words, b_scales, shift, r, c, bias, out_0, out_1, out_2
+):
+    nc = tc.nc
+    with ExitStack() as ctx:
+        keep = ctx.enter_context(tc.tile_pool(name="keep", bufs=1))
+        stage = ctx.enter_context(tc.tile_pool(name="stage", bufs=3))
+        psum = ctx.enter_context(tc.psum_pool(name="psum", bufs=1))
+        ctx.enter_context(tc.manual_schedule())
+
+        def kept(name, shape, dtype):
+            return keep.tile(shape, dtype, name=name, align_bytes=64)
+
+        ident = kept("ident", [P, P], F32)
+        b_raw = kept("b_raw", [P, VG, VG, 2 * GROUP], U8)
+        b_codes = kept("b_codes", [P, VG, 2 * VARS], U8)
+        bs_raw = kept("bs_raw", [P, VG, VARS], U8)
+        b_sc = kept("b_sc", [P, VG, VARS], U8)
+        shift_sb = kept("shift_sb", [P, VG, PACK], BF16)
+        bias_sb = kept("bias_sb", [P, OUTS], BF16)
+        r_raw = kept("r_raw", [P, VG, PACK, VARS], BF16)
+        c_raw = kept("c_raw", [P, VG, PACK, OUTS], BF16)
+        xg = kept("xg", [P, VG, UNITS, PACK], BF16)
+        e32 = kept("e32", [P, VG, PACK, UNITS], F32)
+        xq = kept("xq", [P, VG, UNITS], U32)
+        xs = kept("xs", [P, VG, UNITS], U8)
+        eq = kept("eq", [P, VG, UNITS], U32)
+        es = kept("es", [P, VG, UNITS], U8)
+        zq = kept("zq", [P, UT, VG * P], U32)
+        zs = kept("zs", [P, UT, VG * P], U8)
+        rq = kept("rq", [P, VG, VARS], U32)
+        rs = kept("rs", [P, VG, VARS], U8)
+        cq = kept("cq", [P, VG, OUTS], U32)
+        cs = kept("cs", [P, VG, OUTS], U8)
+        yq = kept("yq", [P, OG, UNITS], U32)
+        ys = kept("ys", [P, OG, UNITS], U8)
+
+        def acc_bank():
+            return psum.tile([P, GROUP], F32, name="acc", bufs=5)
+
+        def turn_bank():
+            return psum.tile([P, GROUP], F32, name="turn", bufs=3)
+
+        def quantize(codes, scales, values):
+            nc.vector.quantize_mx(out=codes.bitcast(FP8X4), scales=scales, in_=values)
+
+        nc.vector.memset(bs_raw[:].rearrange("p g n -> p (g n)").bitcast(I32), 0)
+        make_identity(nc, ident[:])
+
+        def load_b(go):
+            cols = slice(go * 2 * GROUP, (go + 1) * 2 * GROUP)
+            nc.sync.dma_start(
+                out=b_raw[:, go].bitcast(I32),
+                in_=b_words[:, :, cols].rearrange("g p n -> p g n").bitcast(I32),
+            )
+
+        def rows_tile(dtype, width):
+            return stage.tile([P, 2, width], dtype, name="rows", bufs=4)
+
+        x_rows = x.rearrange("(i p) k -> p i k", p=P)
+        x_raw = [rows_tile(BF16, VARS) for pair in range(UT // 2)]
+        load_b(0)
+        nc.sync.dma_start(out=x_raw[0][:], in_=x_rows[:, 0:2, :])
+        for q in range(4):
+            nc.sync.dma_start(
+                out=bs_raw[32 * q : 32 * q + 4, :, :].bitcast(I32),
+                in_=b_scales[:, 4 * q : 4 * q + 4, :].rearrange("g r n -> r g n").bitcast(I32),
+            )
+        for i in range(2, 4):
+            nc.sync.dma_start(out=x_raw[1][:, i % 2, :], in_=x_rows[:, i, :])
+        nc.sync.dma_start(out=shift_sb[:], in_=shift.rearrange("(g p t) -> p g t", p=P, t=PACK))
+        nc.sync.dma_start(out=x_raw[2][:], in_=x_rows[:, 4:6, :])
+        load_b(1)
+        nc.sync.dma_start(out=x_raw[3][:], in_=x_rows[:, 6:8, :])
+
+        def load_r(g):
+            rows = slice(g * GROUP, (g + 1) * GROUP)
+            nc.sync.dma_start(out=r_raw[:, g], in_=r[rows, :].rearrange("(p j) n -> p j n", j=PACK))
+
+        load_r(0)
+        load_r(1)
+        for g in range(VG):
+            rows = slice(g * GROUP, (g + 1) * GROUP)
+            nc.sync.dma_start(out=c_raw[:, g], in_=c[rows, :].rearrange("(p j) n -> p j n", j=PACK))
+        nc.sync.dma_start(out=bias_sb[:], in_=bias.partition_broadcast(P))
+
+        def order_b_codes(g, go):
+            cols = slice(go * 2 * GROUP, (go + 1) * 2 * GROUP)
+            nc.vector.tensor_copy(
+                out=b_codes[:, g, cols].rearrange("p (t m e) -> p t m e", t=PACK, e=2),
+                in_=b_raw[:, go, g, :].rearrange("p (m t e) -> p t m e", t=PACK, e=2),
+            )
+
+        def order_b_scales(go):
+            cols = slice(go * GROUP, (go + 1) * GROUP)
+            nc.vector.tensor_copy(
+                out=b_sc[:, :, cols].rearrange("p g (t m) -> p g t m", t=PACK),
+                in_=bs_raw[:, :, cols].rearrange("p g (m t) -> p g t m", t=PACK),
+            )
+
+        def turn_x(pair, g):
+            bank = turn_bank()[:].rearrange("p (h u) -> p h u", h=2)
+            for a in range(2):
+                words = x_raw[pair][:, a, :].bitcast(F32)
+                for h in range(2):
+                    nc.tensor.transpose(
+                        bank[:, h, a * P : (a + 1) * P], words[:, 256 * g + h : 256 * (g + 1) : 2], ident[:]
+                    )
+            nc.scalar.copy(
+                out=xg[:].bitcast(F32)[:, g, pair * PIECE : (pair + 1) * PIECE, :],
+                in_=bank.rearrange("p h u -> p u h"),
+            )
+
+        def quantize_x(half, g):
+            units = slice(half * HALF, (half + 1) * HALF)
+            quantize(xq[:, g, units], xs[:, g, units], xg[:, g, units, :].rearrange("p u t -> p (u t)"))
+
+        def noise(half, go, t):
+            units = slice(half * HALF, (half + 1) * HALF)
+            col = (go * PACK + t) * P
+            bank = acc_bank()
+            for g in range(VG):
+                nc.tensor.matmul_mx(
+                    out=bank[:],
+                    lhsT=b_codes[:, g, 2 * col : 2 * (col + P)].bitcast(FP4X4),
+                    lhsT_scale=b_sc[:, g, col : col + P],
+                    rhs=xq[:, g, units].bitcast(FP8X4),
+                    rhs_scale=xs[:, g, units],
+                    start=(g == 0),
+                    stop=(g == VG - 1),
+                )
+            nc.vector.scalar_tensor_tensor(
+                out=e32[:, go, t, units],
+                in0=xg[:, go, units, t],
+                scalar=shift_sb[:, go, t : t + 1],
+                in1=bank[:],
+                op0=ADD,
+                op1=SUB,
+            )
+
+        def interleave(engine, dst, src):
+            if engine == "scalar":
+                nc.scalar.copy(out=dst, in_=src)
+            elif engine == "vector":
+                nc.vector.tensor_copy(out=dst, in_=src)
+            else:
+                nc.gpsimd.tensor_scalar(out=dst, in0=src, scalar1=1.0, scalar2=0.0, op0=MULT, op1=ADD)
+
+        staged = {}
+
+        def piece_tile(engine):
+            bufs = 1 if engine == "gpsimd" else 4
+            return stage.tile([P, PIECE * PACK], BF16, name="piece_" + engine, bufs=bufs, align_bytes=64)
+
+        def lay(engine, key):
+            kind, g, n = key
+            cols = slice(n * PIECE, (n + 1) * PIECE)
+            tile = piece_tile(engine)
+            if kind == "e":
+                dst = tile[:].rearrange("p (u i t) -> p u t i", i=2, t=PACK)
+                src = e32[:, g, :, cols].rearrange("p t (u i) -> p u t i", i=2)
+            elif kind == "r":
+                go, t0 = n // 2, 2 * (n % 2)
+                dst = tile[:].rearrange("p (t m j) -> p t m j", t=2, j=PACK)
+                src = r_raw[:, g, :, go * GROUP : (go + 1) * GROUP].rearrange("p j (m t) -> p t m j", t=PACK)
+                src = src[:, t0 : t0 + 2]
+            else:
+                dst = tile[:].rearrange("p (n i j) -> p n j i", i=4, j=PACK)
+                src = c_raw[:, g, :, cols].rearrange("p j (n i) -> p n j i", i=4)
+            interleave(engine, dst, src)
+            staged[key] = tile
+
+        def quantize_piece(key):
+            kind, g, n = key
+            cols = slice(n * PIECE, (n + 1) * PIECE)
+            codes, scales = {"e": (eq, es), "r": (rq, rs), "c": (cq, cs)}[kind]
+            quantize(codes[:, g, cols], scales[:, g, cols], staged[key][:])
+
+        def counterfactual(ut, go):
+            units = slice(ut * P, (ut + 1) * P)
+            bank = acc_bank()[:].rearrange("p (t u) -> p t u", t=PACK)
+            for t in range(PACK):
+                col = (go * PACK + t) * P
+                for g in range(VG):
+                    nc.tensor.matmul_mx(
+                        out=bank[:, t, :],
+                        lhsT=rq[:, g, col : col + P].bitcast(FP8X4),
+                        lhsT_scale=rs[:, g, col : col + P],
+                        rhs=eq[:, g, units].bitcast(FP8X4),
+                        rhs_scale=es[:, g, units],
+                        start=(g == 0),
+                        stop=(g == VG - 1),
+                    )
+            if go == 0:
+                staged["z", ut] = stage.tile([P, VG, GROUP], BF16, name="zg", bufs=5, align_bytes=64)
+            nc.vector.tensor_tensor(
+                out=staged["z", ut][:, go, :].rearrange("p (u i t) -> p u t i", i=2, t=PACK),
+                in0=bank.rearrange("p t (u i) -> p u t i", i=2),
+                in1=e32[:, go, :, units].rearrange("p t (u i) -> p u t i", i=2),
+                op=ADD,
+            )
+
+        def quantize_z(ut):
+            quantize(zq[:, ut, :], zs[:, ut, :], staged["z", ut][:].rearrange("p g n -> p (g n)"))
+
+        def outcome(oc, ut):
+            cols = slice(oc * GROUP, (oc + 1) * GROUP)
+            pair, a = divmod(ut, 2)
+            bank = acc_bank()
+            for g in range(VG):
+                nc.tensor.matmul_mx(
+                    out=bank[:],
+                    lhsT=zq[:, ut, g * P : (g + 1) * P].bitcast(FP8X4),
+                    lhsT_scale=zs[:, ut, g * P : (g + 1) * P],
+                    rhs=cq[:, g, cols].bitcast(FP8X4),
+                    rhs_scale=cs[:, g, cols],
+                    start=(g == 0),
+                    stop=(g == VG - 1),
+                )
+            if a == 0:
+                staged["y", oc, pair] = rows_tile(F32, GROUP)
+            nc.vector.tensor_tensor(out=staged["y", oc, pair][:, a, :], in0=bank[:], in1=bias_sb[:, cols], op=ADD)
+
+        def store_y(oc, pair, tiles=slice(0, 2)):
+            rows = out_0[pair * 2 * P : (pair + 1) * 2 * P, oc * GROUP : (oc + 1) * GROUP]
+            nc.sync.dma_start(
+                out=rows.rearrange("(a p) o -> p a o", p=P)[:, tiles, :], in_=staged["y", oc, pair][:, tiles, :]
+            )
+
+        def round_y(engine, oc, pair, tiles=slice(0, 2)):
+            if tiles.start == 0:
+                staged["y16", oc, pair] = stage.tile([P, 2, 2 * P, 2], BF16, name="y16", bufs=4)
+            units = slice(tiles.start * P, tiles.stop * P)
+            src = staged["y", oc, pair][:].rearrange("p a (m h e) -> p h (a m) e", h=2, e=2)
+            interleave(engine, staged["y16", oc, pair][:, :, units, :], src[:, :, units, :])
+
+        def turn_y(oc, pair, tiles=slice(0, 2)):
+            words = staged["y16", oc, pair][:].rearrange("p h n e -> p h (n e)").bitcast(F32)
+            bank = turn_bank()[:].rearrange("p (h u) -> p h u", h=2)
+            for a in range(tiles.start, tiles.stop):
+                for h in range(2):
+                    nc.tensor.transpose(bank[:, h, a * P : (a + 1) * P], words[:, h, a * P : (a + 1) * P], ident[:])
+            staged["yb", oc, pair, tiles.start] = bank
+
+        def group_y(oc, pair, tiles=slice(0, 2)):
+            if tiles.start == 0:
+                staged["yg", oc, pair] = stage.tile([P, PIECE * PACK], BF16, name="yg", bufs=4, align_bytes=64)
+            units = slice(tiles.start * P, tiles.stop * P)
+            nc.scalar.copy(
+                out=staged["yg", oc, pair][:].bitcast(F32).rearrange("p (u h) -> p u h", h=2)[:, units, :],
+                in_=staged["yb", oc, pair, tiles.start].rearrange("p h u -> p u h")[:, units, :],
+            )
+
+        def quantize_y(oc, pair, tiles=slice(0, 2)):
+            units = slice(pair * PIECE + tiles.start * P, pair * PIECE + tiles.stop * P)
+            values = staged["yg", oc, pair][:, tiles.start * GROUP : tiles.stop * GROUP]
+            quantize(yq[:, oc, units], ys[:, oc, units], values)
+
+        def store_words(oc, first, last):
+            units = slice(first * PIECE, (last + 1) * PIECE)
+            nc.sync.dma_start(
+                out=out_1[oc].rearrange("p m t -> p (m t)").bitcast(I32)[:, units],
+                in_=yq[:, oc, units].bitcast(I32),
+            )
+
+        def store_scales(queues, groups):
+            for q in range(4):
+                queues[q % len(queues)].dma_start(
+                    out=out_2[groups, 4 * q : 4 * q + 4, :].rearrange("g r n -> r g n").bitcast(I32),
+                    in_=ys[32 * q : 32 * q + 4, groups, :].bitcast(I32),
+                )
+
+        S, G, V = "scalar", "gpsimd", "vector"
+        order_b_codes(0, 0)
+        order_b_codes(1, 0)
+        order_b_scales(0)
+        order_b_scales(1)
+        for pair in range(3):
+            for g in range(VG):
+                turn_x(pair, g)
+        quantize_x(0, 0)
+        quantize_x(0, 1)
+        order_b_codes(0, 1)
+        order_b_codes(1, 1)
+        noise(0, 0, 0)
+        noise(0, 0, 1)
+        for g in range(VG):
+            turn_x(3, g)
+        lay(G, ("r", 0, 0))
+        noise(0, 0, 2)
+        noise(0, 0, 3)
+        lay(S, ("r", 0, 1))
+        lay(S, ("e", 0, 0))
+        lay(S, ("e", 0, 1))
+        quantize_x(1, 0)
+        quantize_x(1, 1)
+        quantize_piece(("r", 0, 0))
+        lay(G, ("r", 0, 2))
+        noise(0, 1, 0)
+        noise(0, 1, 1)
+        noise(0, 1, 2)
+        quantize_piece(("r", 0, 1))
+        quantize_piece(("r", 0, 2))
+        lay(G, ("r", 1, 0))
+        noise(0, 1, 3)
+        lay(S, ("e", 1, 0))
+        lay(S, ("e", 1, 1))
+        noise(1, 0, 0)
+        noise(1, 0, 1)
+        quantize_piece(("e", 0, 0))
+        quantize_piece(("e", 0, 1))
+        quantize_piece(("r", 1, 0))
+        lay(G, ("r", 1, 1))
+        lay(S, ("r", 0, 3))
+        noise(1, 0, 2)
+        noise(1, 0, 3)
+        lay(S, ("r", 1, 2))
+        lay(S, ("e", 0, 2))
+        noise(1, 1, 0)
+        quantize_piece(("e", 1, 0))
+        quantize_piece(("e", 1, 1))
+        quantize_piece(("r", 1, 1))
+        lay(G, ("r", 1, 3))
+        noise(1, 1, 1)
+        noise(1, 1, 2)
+        noise(1, 1, 3)
+        quantize_piece(("r", 0, 3))
+        quantize_piece(("r", 1, 2))
+        quantize_piece(("r", 1, 3))
+        lay(G, ("c", 0, 0))
+        lay(S, ("e", 1, 2))
+        lay(S, ("e", 0, 3))
+        lay(S, ("e", 1, 3))
+        counterfactual(0, 0)
+        counterfactual(1, 0)
+        counterfactual(2, 0)
+        quantize_piece(("e", 0, 2))
+        quantize_piece(("e", 1, 2))
+        quantize_piece(("c", 0, 0))
+        lay(G, ("c", 1, 0))
+        lay(S, ("c", 0, 1))
+        lay(S, ("c", 1, 1))
+        counterfactual(0, 1)
+        counterfactual(1, 1)
+        counterfactual(2, 1)
+        quantize_piece(("e", 0, 3))
+        quantize_piece(("e", 1, 3))
+        quantize_z(0)
+        quantize_z(1)
+        quantize_piece(("c", 1, 0))
+        lay(G, ("c", 0, 2))
+        lay(S, ("c", 1, 2))
+        counterfactual(3, 0)
+        counterfactual(3, 1)
+        counterfactual(4, 0)
+        quantize_piece(("c", 0, 1))
+        quantize_piece(("c", 1, 1))
+        quantize_z(2)
+        quantize_z(3)
+        quantize_piece(("c", 0, 2))
+
+        units = [(oc, pair) for oc, half in ((0, 0), (1, 0), (0, 1), (1, 1), (2, 0), (2, 1)) for pair in (2 * half, 2 * half + 1)]
+        late = [("c", 0, 3), ("c", 0, 4), ("c", 1, 4), ("c", 0, 5), ("c", 1, 5)]
+
+        def outcomes(n):
+            oc, pair = units[n]
+            outcome(oc, 2 * pair)
+            outcome(oc, 2 * pair + 1)
+            store_y(oc, pair)
+
+        done = set()
+
+        def finish(n):
+            oc, pair = units[n]
+            quantize_y(oc, pair)
+            done.add(n)
+            if n ^ 1 in done:
+                store_words(oc, pair & 2, pair | 1)
+
+        def turn_and_group(n):
+            turn_y(*units[n])
+            group_y(*units[n])
+
+        lay(S, ("c", 1, 3))
+        for n in range(4):
+            lay(G, late[n])
+            counterfactual(4 + n, 1)
+            if n < 3:
+                counterfactual(5 + n, 0)
+            outcomes(n)
+            if n >= 2:
+                turn_and_group(n - 2)
+            round_y(S, *units[n])
+            if n == 0:
+                quantize_piece(("c", 1, 2))
+            if n == 1:
+                quantize_piece(("c", 1, 3))
+            if n >= 3:
+                finish(n - 3)
+            quantize_z(4 + n)
+            quantize_piece(late[n])
+        lay(G, late[4])
+        for n in range(4, 10, 2):
+            outcomes(n)
+            round_y(S, *units[n])
+            outcomes(n + 1)
+            turn_and_group(n - 2)
+            turn_and_group(n - 1)
+            round_y(S, *units[n + 1])
+            finish(n - 3)
+            if n > 4:
+                finish(n - 4)
+            if n == 4:
+                quantize_piece(late[4])
+        outcomes(10)
+        turn_and_group(8)
+        finish(6)
+        finish(7)
+        store_scales([nc.sync], slice(0, 2))
+        round_y(V, *units[10])
+        oc, pair = units[11]
+        outcome(oc, 2 * pair)
+        outcome(oc, 2 * pair + 1)
+        turn_and_group(9)
+        for a in range(2):
+            tiles = slice(a, a + 1)
+            store_y(oc, pair, tiles)
+            round_y(V, oc, pair, tiles)
+        turn_and_group(10)
+        finish(8)
+        finish(9)
+        for a in range(2):
+            tiles = slice(a, a + 1)
+            turn_y(oc, pair, tiles)
+            group_y(oc, pair, tiles)
+        quantize_y(*units[10])
+        for a in range(2):
+            quantize_y(oc, pair, slice(a, a + 1))
+        store_words(oc, pair - 1, pair)
+        store_scales([nc.scalar, nc.sync], slice(2, 3))

@@ -16,6 +16,7 @@ FP4X4 = mybir.dt.float4_e2m1fn_x4
 ADD = mybir.AluOpType.add
 SUB = mybir.AluOpType.subtract
 MULT = mybir.AluOpType.mult
+IDENTITY = mybir.ActivationFunctionType.Identity
 
 P = 128
 PACK = 4
@@ -25,6 +26,77 @@ OG = OUTS // GROUP
 UT = UNITS // P
 HALF = 512
 PIECE = 256
+TURNED = (0,)
+FIRST = 1
+ORDER = [
+    ("tx", "P", 0, 1), ("xo", "S", 0, 1), ("pc", "V", 0, 0), ("pc", "V", 1, 0),
+    ("tx", "P", 0, 0), ("ps", "V", 0), ("tx", "P", 1, 0), ("xo", "S", 0, 0),
+    ("ps", "V", 1), ("qx", "V", 1, 0, 1), ("tx", "P", 1, 1), ("qx", "V", 0, 0, 1),
+    ("me", "P", 0, 0, 2), ("lay", "G", "r", 0, 3, 1), ("xo", "S", 1, 0), ("xo", "S", 1, 1),
+    ("me", "P", 0, 0, 0), ("pc", "V", 0, 1), ("lay", "S", "r", 0, 1, 1), ("qx", "V", 0, 1, 1),
+    ("qx", "V", 1, 1, 1), ("pc", "V", 1, 1), ("me", "P", 1, 0, 2), ("lay", "S", "r", 0, 0, 1),
+    ("tx", "P", 2, 0), ("ee", "V", 0, 0, 2), ("ee", "V", 0, 0, 0), ("ee", "V", 1, 0, 2),
+    ("qp", "V", "r", 0, 3), ("tx", "P", 3, 0), ("xo", "S", 2, 0), ("me", "P", 0, 1, 2),
+    ("lay", "V", "e", 0, 0, 1), ("tx", "P", 2, 1), ("tx", "P", 3, 1), ("me", "P", 0, 1, 0),
+    ("qp", "V", "r", 0, 0), ("ee", "V", 0, 1, 2), ("lay", "S", "r", 0, 2, 1), ("me", "P", 1, 0, 0),
+    ("xo", "S", 3, 0), ("qp", "V", "r", 0, 1), ("qp", "V", "r", 0, 2), ("qp", "V", "e", 0, 0),
+    ("qx", "V", 0, 2, 2), ("xo", "S", 2, 1), ("xo", "S", 3, 1), ("ee", "V", 0, 1, 0),
+    ("qx", "V", 1, 2, 2), ("me", "P", 1, 1, 0), ("lay", "S", "r", 1, 0, 2), ("me", "P", 1, 1, 2),
+    ("ee", "V", 1, 0, 0), ("m1", "P", 1, 1, 3), ("ee", "V", 1, 1, 0), ("m1", "P", 1, 1, 1),
+    ("lay", "S", "r", 1, 2, 2), ("m1", "P", 1, 1, 2), ("ee", "V", 1, 1, 2), ("lay", "S", "e", 1, 1, 1),
+    ("qp", "V", "r", 1, 0), ("lay", "G", "e", 1, 0, 1), ("lay", "S", "c", 1, 0, 2), ("qp", "V", "e", 1, 0),
+    ("m1", "P", 1, 1, 0), ("lay", "G", "e", 0, 1, 1), ("e1", "V", 1, 1, 3), ("m1", "P", 1, 0, 3),
+    ("e1", "V", 1, 1, 1), ("e1", "V", 1, 1, 2), ("e1", "V", 1, 1, 0), ("m1", "P", 1, 0, 2),
+    ("qp", "V", "r", 1, 2), ("m1", "P", 1, 0, 0), ("qp", "V", "e", 0, 1), ("m1", "P", 1, 0, 1),
+    ("qp", "V", "e", 1, 1), ("m2", "P", 0, 1), ("lay", "S", "e", 1, 2, 2), ("e1", "V", 1, 0, 3),
+    ("e1", "V", 1, 0, 2), ("e1", "V", 1, 0, 0), ("m2", "P", 3, 1), ("m2", "P", 1, 1),
+    ("m2", "P", 0, 0), ("z", "V", 0, 1), ("lay", "G", "c", 0, 0, 1), ("e1", "V", 1, 0, 1),
+    ("m2", "P", 2, 1), ("m2", "P", 3, 0), ("z", "V", 3, 1), ("z", "V", 1, 1),
+    ("z", "V", 0, 0), ("qz", "V", 1, 0, 1), ("z", "V", 2, 1), ("lay", "S", "e", 0, 2, 2),
+    ("qp", "V", "e", 1, 2), ("qp", "V", "c", 1, 0), ("m2", "P", 1, 0), ("qp", "V", "e", 0, 2),
+    ("m2", "P", 2, 0), ("m2", "P", 4, 1), ("qp", "V", "c", 0, 0), ("z", "V", 3, 0),
+    ("lay", "G", "c", 0, 2, 1), ("m2", "P", 5, 1), ("z", "V", 1, 0), ("z", "V", 4, 1),
+    ("m2", "P", 7, 1), ("z", "V", 2, 0), ("m2", "P", 4, 0), ("qz", "V", 1, 1, 1),
+    ("qz", "V", 0, 0, 1), ("qz", "V", 0, 1, 1), ("z", "V", 5, 1), ("lay", "S", "c", 0, 1, 1),
+    ("m2", "P", 6, 0), ("mA", "P", 0, 0, 0), ("z", "V", 7, 1), ("lay", "S", "c", 1, 2, 2),
+    ("mA", "P", 0, 0, 1), ("lay", "S", "c", 1, 4, 2), ("m2", "P", 6, 1), ("z", "V", 4, 0),
+    ("qp", "V", "c", 0, 1), ("m2", "P", 5, 0), ("aA", "S", 0, 0, 0), ("z", "V", 6, 0),
+    ("mA", "P", 0, 0, 3), ("lay", "S", "c", 0, 3, 1), ("qp", "V", "c", 1, 2), ("z", "V", 6, 1),
+    ("mA", "P", 0, 0, 2), ("aA", "S", 0, 0, 1), ("qp", "V", "c", 0, 3), ("aA", "S", 0, 0, 3),
+    ("aA", "S", 0, 0, 2), ("lay", "S", "c", 0, 4, 1), ("qp", "V", "c", 0, 2), ("qz", "V", 1, 2, 2),
+    ("z", "V", 5, 0), ("m2", "P", 7, 0), ("z", "V", 7, 0), ("m3", "P", 1, 2),
+    ("tb", "P", 0, 0, 0), ("tb", "P", 0, 0, 1), ("lay", "G", "c", 0, 5, 1), ("m3", "P", 1, 0),
+    ("rb", "S", 0, 0, 0), ("y", "V", 1, 2), ("m3", "P", 1, 3), ("rb", "S", 0, 0, 1),
+    ("m3", "P", 1, 1), ("qz", "V", 0, 2, 2), ("lay", "S", "y", 0, 1, 1), ("m3", "P", 1, 4),
+    ("qp", "V", "c", 0, 5), ("qp", "V", "c", 0, 4), ("y", "V", 1, 3), ("mA", "P", 0, 1, 0),
+    ("st", "D", 0, 0), ("y", "V", 1, 0), ("tb", "P", 0, 1, 0), ("tb", "P", 0, 1, 1),
+    ("m3", "P", 1, 5), ("y", "V", 1, 4), ("y", "V", 1, 1), ("cast", "S", 1, 1),
+    ("qp", "V", "c", 1, 4), ("mA", "P", 0, 1, 3), ("aA", "S", 0, 1, 0), ("mA", "P", 0, 1, 2),
+    ("lay", "G", "y", 0, 0, 1), ("m3", "P", 2, 0), ("rb", "S", 0, 1, 0), ("rb", "S", 0, 1, 1),
+    ("st", "D", 1, 1), ("m3", "P", 2, 1), ("cast", "G", 1, 0), ("aA", "S", 0, 1, 2),
+    ("y", "V", 1, 5), ("st", "D", 1, 0), ("m3", "P", 2, 4), ("aA", "V", 0, 1, 3),
+    ("cast", "S", 1, 2), ("y", "V", 2, 0), ("st", "D", 1, 2), ("mA", "P", 0, 1, 1),
+    ("aA", "S", 0, 1, 1), ("qp", "V", "y", 0, 1), ("m3", "P", 2, 5), ("y", "V", 2, 1),
+    ("m3", "P", 1, 6), ("y", "V", 2, 4), ("cast", "S", 2, 0), ("m3", "P", 1, 7),
+    ("m3", "P", 2, 2), ("qp", "V", "y", 0, 0), ("st", "D", 0, 1), ("ty", "P", 1, 0),
+    ("lay", "S", "y", 0, 3, 1), ("m3", "P", 2, 3), ("tb", "P", 0, 2, 0), ("y", "V", 2, 5),
+    ("y", "V", 1, 6), ("y", "V", 1, 7), ("st", "D", 2, 0), ("ty", "P", 1, 1),
+    ("y", "V", 2, 2), ("sw", "D", 0, 0, 2), ("gy", "S", 1, 0), ("rb", "S", 0, 2, 0),
+    ("lay", "G", "y", 0, 2, 1), ("tb", "P", 0, 2, 1), ("qp", "V", "y", 0, 2), ("gy", "S", 1, 1),
+    ("qp", "V", "y", 0, 3), ("y", "V", 2, 3), ("m3", "P", 2, 6), ("cast", "V", 1, 3),
+    ("cast", "S", 2, 2), ("st", "D", 2, 2), ("ty", "P", 1, 2), ("ty", "P", 1, 3),
+    ("st", "D", 1, 3), ("gy", "S", 1, 2), ("rb", "V", 0, 2, 1), ("gy", "S", 1, 3),
+    ("ty", "P", 2, 0), ("m3", "P", 2, 7), ("tb", "P", 0, 3, 0), ("tb", "P", 0, 3, 1),
+    ("sw", "D", 0, 2, 2), ("qy", "V", 1, 0, 4), ("rb", "S", 0, 3, 0), ("y", "V", 2, 6),
+    ("gy", "V", 2, 0), ("rb", "S", 0, 3, 1), ("y", "V", 2, 7), ("st", "D", 2, 1),
+    ("st", "D", 0, 2), ("st1", "D", 0), ("cast", "G", 2, 1), ("qy", "V", 1, 4, 4),
+    ("cast1", "V", 0), ("sw", "D", 1, 0, 2), ("ty", "P", 2, 1), ("gy", "V", 2, 1),
+    ("cast1", "V", 1), ("st1", "D", 1), ("sw", "D", 1, 2, 2), ("ty", "P", 2, 2),
+    ("ss", "D", 0), ("qy", "V", 2, 0, 4), ("gy", "S", 2, 2), ("ty1", "P", 0),
+    ("st", "D", 0, 3), ("ty1", "P", 1), ("qy", "V", 2, 4, 2), ("gy1", "S", 0),
+    ("qy1", "V", 0), ("gy1", "S", 1), ("qy1", "V", 1), ("sw", "D", 2, 0, 2),
+    ("sw", "D", 2, 2, 1), ("ss", "D", 1), ("sw", "D", 2, 3, 1),
+]
 
 
 def tile_structural_model_counterfactual_k1_kernel(
@@ -46,8 +118,8 @@ def tile_structural_model_counterfactual_k1_kernel(
         bs_raw = kept("bs_raw", [P, VG, VARS], U8)
         b_sc = kept("b_sc", [P, VG, VARS], U8)
         shift_sb = kept("shift_sb", [P, VG, PACK], BF16)
-        bias_sb = kept("bias_sb", [P, OUTS], BF16)
-        r_raw = kept("r_raw", [P, VG, PACK, VARS], BF16)
+        bias_col = kept("bias_col", [P, PACK], BF16)
+        bias_sb = kept("bias_sb", [P, OUTS - GROUP], BF16)
         c_raw = kept("c_raw", [P, VG, PACK, OUTS], BF16)
         xg = kept("xg", [P, VG, UNITS, PACK], BF16)
         e32 = kept("e32", [P, VG, PACK, UNITS], F32)
@@ -55,8 +127,8 @@ def tile_structural_model_counterfactual_k1_kernel(
         xs = kept("xs", [P, VG, UNITS], U8)
         eq = kept("eq", [P, VG, UNITS], U32)
         es = kept("es", [P, VG, UNITS], U8)
-        zq = kept("zq", [P, UT, VG * P], U32)
-        zs = kept("zs", [P, UT, VG * P], U8)
+        zq = kept("zq", [P, VG, UNITS], U32)
+        zs = kept("zs", [P, VG, UNITS], U8)
         rq = kept("rq", [P, VG, VARS], U32)
         rs = kept("rs", [P, VG, VARS], U8)
         cq = kept("cq", [P, VG, OUTS], U32)
@@ -98,36 +170,66 @@ def tile_structural_model_counterfactual_k1_kernel(
         for i in range(2, 4):
             nc.sync.dma_start(out=x_raw[1][:, i % 2, :], in_=x_rows[:, i, :])
         nc.sync.dma_start(out=shift_sb[:], in_=shift.rearrange("(g p t) -> p g t", p=P, t=PACK))
-        nc.sync.dma_start(out=x_raw[2][:], in_=x_rows[:, 4:6, :])
         load_b(1)
-        nc.sync.dma_start(out=x_raw[3][:], in_=x_rows[:, 6:8, :])
 
-        def load_r(g):
+        def wide_tile(dtype, width):
+            return stage.tile([P, PACK, width], dtype, name="wide", bufs=2)
+
+        r_raw = [wide_tile(BF16, VARS) for g in range(VG)]
+        for g in range(VG):
             rows = slice(g * GROUP, (g + 1) * GROUP)
-            nc.sync.dma_start(out=r_raw[:, g], in_=r[rows, :].rearrange("(p j) n -> p j n", j=PACK))
-
-        load_r(0)
-        load_r(1)
+            nc.sync.dma_start(out=r_raw[g][:], in_=r[rows, :].rearrange("(p j) n -> p j n", j=PACK))
+            if g == 0:
+                nc.sync.dma_start(out=x_raw[2][:], in_=x_rows[:, 4:6, :])
+                nc.sync.dma_start(out=x_raw[3][:], in_=x_rows[:, 6:8, :])
         for g in range(VG):
             rows = slice(g * GROUP, (g + 1) * GROUP)
             nc.sync.dma_start(out=c_raw[:, g], in_=c[rows, :].rearrange("(p j) n -> p j n", j=PACK))
-        nc.sync.dma_start(out=bias_sb[:], in_=bias.partition_broadcast(P))
+        nc.sync.dma_start(out=bias_col[:], in_=bias[0:GROUP].rearrange("(p t) -> p t", t=PACK))
+        nc.sync.dma_start(out=bias_sb[:], in_=bias[GROUP:OUTS].partition_broadcast(P))
 
-        def order_b_codes(g, go):
+        staged = {}
+
+        def move(engine, dst, src):
+            if engine == "S":
+                nc.scalar.copy(out=dst, in_=src)
+            elif engine == "V":
+                nc.vector.tensor_copy(out=dst, in_=src)
+            else:
+                nc.gpsimd.tensor_scalar(out=dst, in0=src, scalar1=1.0, scalar2=0.0, op0=MULT, op1=ADD)
+
+        def piece_tile(engine):
+            if engine == "G":
+                return stage.tile([P, PIECE * PACK], BF16, name="piece_gpsimd", bufs=1, align_bytes=64)
+            return stage.tile([P, 2 * PIECE * PACK], BF16, name="piece", bufs=5, align_bytes=64)
+
+        def mx_group(out, lhsT, lhsT_scale, rhs, rhs_scale):
+            for g in range(VG):
+                nc.tensor.matmul_mx(
+                    out=out,
+                    lhsT=lhsT(g),
+                    lhsT_scale=lhsT_scale(g),
+                    rhs=rhs(g),
+                    rhs_scale=rhs_scale(g),
+                    start=(g == 0),
+                    stop=(g == VG - 1),
+                )
+
+        def pc(engine, g, go):
             cols = slice(go * 2 * GROUP, (go + 1) * 2 * GROUP)
             nc.vector.tensor_copy(
                 out=b_codes[:, g, cols].rearrange("p (t m e) -> p t m e", t=PACK, e=2),
                 in_=b_raw[:, go, g, :].rearrange("p (m t e) -> p t m e", t=PACK, e=2),
             )
 
-        def order_b_scales(go):
+        def ps(engine, go):
             cols = slice(go * GROUP, (go + 1) * GROUP)
             nc.vector.tensor_copy(
                 out=b_sc[:, :, cols].rearrange("p g (t m) -> p g t m", t=PACK),
                 in_=bs_raw[:, :, cols].rearrange("p g (m t) -> p g t m", t=PACK),
             )
 
-        def turn_x(pair, g):
+        def tx(engine, pair, g):
             bank = turn_bank()[:].rearrange("p (h u) -> p h u", h=2)
             for a in range(2):
                 words = x_raw[pair][:, a, :].bitcast(F32)
@@ -135,135 +237,202 @@ def tile_structural_model_counterfactual_k1_kernel(
                     nc.tensor.transpose(
                         bank[:, h, a * P : (a + 1) * P], words[:, 256 * g + h : 256 * (g + 1) : 2], ident[:]
                     )
-            nc.scalar.copy(
-                out=xg[:].bitcast(F32)[:, g, pair * PIECE : (pair + 1) * PIECE, :],
-                in_=bank.rearrange("p h u -> p u h"),
+            staged["tx", pair, g] = bank
+
+        def xo(engine, pair, g):
+            move(
+                engine,
+                xg[:].bitcast(F32)[:, g, pair * PIECE : (pair + 1) * PIECE, :],
+                staged["tx", pair, g].rearrange("p h u -> p u h"),
             )
 
-        def quantize_x(half, g):
-            units = slice(half * HALF, (half + 1) * HALF)
+        def qx(engine, g, first, count):
+            units = slice(first * PIECE, (first + count) * PIECE)
             quantize(xq[:, g, units], xs[:, g, units], xg[:, g, units, :].rearrange("p u t -> p (u t)"))
 
-        def noise(half, go, t):
-            units = slice(half * HALF, (half + 1) * HALF)
+        def parents(out, go, t, units):
             col = (go * PACK + t) * P
-            bank = acc_bank()
-            for g in range(VG):
-                nc.tensor.matmul_mx(
-                    out=bank[:],
-                    lhsT=b_codes[:, g, 2 * col : 2 * (col + P)].bitcast(FP4X4),
-                    lhsT_scale=b_sc[:, g, col : col + P],
-                    rhs=xq[:, g, units].bitcast(FP8X4),
-                    rhs_scale=xs[:, g, units],
-                    start=(g == 0),
-                    stop=(g == VG - 1),
-                )
+            mx_group(
+                out,
+                lambda g: b_codes[:, g, 2 * col : 2 * (col + P)].bitcast(FP4X4),
+                lambda g: b_sc[:, g, col : col + P],
+                lambda g: xq[:, g, units].bitcast(FP8X4),
+                lambda g: xs[:, g, units],
+            )
+
+        def noise_from(bank, go, t, units):
             nc.vector.scalar_tensor_tensor(
                 out=e32[:, go, t, units],
                 in0=xg[:, go, units, t],
                 scalar=shift_sb[:, go, t : t + 1],
-                in1=bank[:],
+                in1=bank,
                 op0=ADD,
                 op1=SUB,
             )
 
-        def interleave(engine, dst, src):
-            if engine == "scalar":
-                nc.scalar.copy(out=dst, in_=src)
-            elif engine == "vector":
-                nc.vector.tensor_copy(out=dst, in_=src)
+        def me(engine, pair, go, t0):
+            bank = acc_bank()[:].rearrange("p (t u) -> p t u", t=2)
+            for t in range(2):
+                for a in range(2):
+                    ut = 2 * pair + a
+                    parents(bank[:, t, a * P : (a + 1) * P], go, t0 + t, slice(ut * P, (ut + 1) * P))
+            staged["me", pair, go, t0] = bank
+
+        def ee(engine, pair, go, t0):
+            for t in range(2):
+                noise_from(
+                    staged["me", pair, go, t0][:, t, :], go, t0 + t, slice(pair * PIECE, (pair + 1) * PIECE)
+                )
+
+        def m1(engine, half, go, t):
+            bank = acc_bank()
+            parents(bank[:], go, t, slice(half * HALF, (half + 1) * HALF))
+            staged["m1", half, go, t] = bank
+
+        def e1(engine, half, go, t):
+            noise_from(staged["m1", half, go, t][:], go, t, slice(half * HALF, (half + 1) * HALF))
+
+        def lay(engine, kind, g, first, count):
+            cols = slice(first * PIECE, (first + count) * PIECE)
+            tile = piece_tile(engine)[:, : count * PIECE * PACK]
+            if kind in "ey":
+                if kind == "e":
+                    rows = e32[:, g, :, cols]
+                else:
+                    rows = staged["yt", g, first // 2][:, :, (first % 2) * PIECE : (first % 2 + count) * PIECE]
+                if engine == "G":
+                    dst = tile.rearrange("p (u t) -> p u t", t=PACK)
+                    src = rows.rearrange("p t u -> p u t")
+                else:
+                    dst = tile.rearrange("p (u i t) -> p u t i", i=2, t=PACK)
+                    src = rows.rearrange("p t (u i) -> p u t i", i=2)
+            elif kind == "r" or first // 2 in TURNED:
+                raw = r_raw[g] if kind == "r" else c_raw[:, g]
+                group, t0 = first // 2, 2 * (first % 2)
+                dst = tile.rearrange("p (t m j) -> p t m j", m=P, j=PACK)
+                src = raw[:, :, group * GROUP : (group + 1) * GROUP].rearrange("p j (m t) -> p t m j", t=PACK)
+                src = src[:, t0 : t0 + 2 * count]
+            elif engine == "G":
+                dst = tile.rearrange("p (n j) -> p n j", j=PACK)
+                src = c_raw[:, g, :, cols].rearrange("p j n -> p n j")
             else:
-                nc.gpsimd.tensor_scalar(out=dst, in0=src, scalar1=1.0, scalar2=0.0, op0=MULT, op1=ADD)
-
-        staged = {}
-
-        def piece_tile(engine):
-            bufs = 1 if engine == "gpsimd" else 4
-            return stage.tile([P, PIECE * PACK], BF16, name="piece_" + engine, bufs=bufs, align_bytes=64)
-
-        def lay(engine, key):
-            kind, g, n = key
-            cols = slice(n * PIECE, (n + 1) * PIECE)
-            tile = piece_tile(engine)
-            if kind == "e":
-                dst = tile[:].rearrange("p (u i t) -> p u t i", i=2, t=PACK)
-                src = e32[:, g, :, cols].rearrange("p t (u i) -> p u t i", i=2)
-            elif kind == "r":
-                go, t0 = n // 2, 2 * (n % 2)
-                dst = tile[:].rearrange("p (t m j) -> p t m j", t=2, j=PACK)
-                src = r_raw[:, g, :, go * GROUP : (go + 1) * GROUP].rearrange("p j (m t) -> p t m j", t=PACK)
-                src = src[:, t0 : t0 + 2]
-            else:
-                dst = tile[:].rearrange("p (n i j) -> p n j i", i=4, j=PACK)
+                dst = tile.rearrange("p (n i j) -> p n j i", i=4, j=PACK)
                 src = c_raw[:, g, :, cols].rearrange("p j (n i) -> p n j i", i=4)
-            interleave(engine, dst, src)
-            staged[key] = tile
+            move(engine, dst, src)
+            staged["piece", kind, g, first] = (tile, cols)
 
-        def quantize_piece(key):
-            kind, g, n = key
-            cols = slice(n * PIECE, (n + 1) * PIECE)
-            codes, scales = {"e": (eq, es), "r": (rq, rs), "c": (cq, cs)}[kind]
-            quantize(codes[:, g, cols], scales[:, g, cols], staged[key][:])
+        def qp(engine, kind, g, first):
+            tile, cols = staged["piece", kind, g, first]
+            codes, scales = {"e": (eq, es), "r": (rq, rs), "c": (cq, cs), "y": (yq, ys)}[kind]
+            quantize(codes[:, g, cols], scales[:, g, cols], tile)
 
-        def counterfactual(ut, go):
+        def m2(engine, ut, go):
             units = slice(ut * P, (ut + 1) * P)
             bank = acc_bank()[:].rearrange("p (t u) -> p t u", t=PACK)
             for t in range(PACK):
                 col = (go * PACK + t) * P
-                for g in range(VG):
-                    nc.tensor.matmul_mx(
-                        out=bank[:, t, :],
-                        lhsT=rq[:, g, col : col + P].bitcast(FP8X4),
-                        lhsT_scale=rs[:, g, col : col + P],
-                        rhs=eq[:, g, units].bitcast(FP8X4),
-                        rhs_scale=es[:, g, units],
-                        start=(g == 0),
-                        stop=(g == VG - 1),
-                    )
-            if go == 0:
-                staged["z", ut] = stage.tile([P, VG, GROUP], BF16, name="zg", bufs=5, align_bytes=64)
+                mx_group(
+                    bank[:, t, :],
+                    lambda g: rq[:, g, col : col + P].bitcast(FP8X4),
+                    lambda g: rs[:, g, col : col + P],
+                    lambda g: eq[:, g, units].bitcast(FP8X4),
+                    lambda g: es[:, g, units],
+                )
+            staged["m2", ut, go] = bank
+
+        def z(engine, ut, go):
+            half, a = divmod(ut, 4)
+            if a == 0:
+                staged["z", half, go] = stage.tile([P, 4, GROUP], BF16, name="zg", bufs=3, align_bytes=64)
             nc.vector.tensor_tensor(
-                out=staged["z", ut][:, go, :].rearrange("p (u i t) -> p u t i", i=2, t=PACK),
-                in0=bank.rearrange("p t (u i) -> p u t i", i=2),
-                in1=e32[:, go, :, units].rearrange("p t (u i) -> p u t i", i=2),
+                out=staged["z", half, go][:, a, :].rearrange("p (u i t) -> p u t i", i=2, t=PACK),
+                in0=staged["m2", ut, go].rearrange("p t (u i) -> p u t i", i=2),
+                in1=e32[:, go, :, ut * P : (ut + 1) * P].rearrange("p t (u i) -> p u t i", i=2),
                 op=ADD,
             )
 
-        def quantize_z(ut):
-            quantize(zq[:, ut, :], zs[:, ut, :], staged["z", ut][:].rearrange("p g n -> p (g n)"))
+        def qz(engine, go, first, count):
+            units = slice(first * PIECE, (first + count) * PIECE)
+            tiles = slice(2 * (first % 2), 2 * (first % 2 + count))
+            values = staged["z", first // 2, go][:, tiles, :].rearrange("p a n -> p (a n)")
+            quantize(zq[:, go, units], zs[:, go, units], values)
 
-        def outcome(oc, ut):
+        def m3(engine, oc, ut):
             cols = slice(oc * GROUP, (oc + 1) * GROUP)
-            pair, a = divmod(ut, 2)
+            units = slice(ut * P, (ut + 1) * P)
             bank = acc_bank()
-            for g in range(VG):
-                nc.tensor.matmul_mx(
-                    out=bank[:],
-                    lhsT=zq[:, ut, g * P : (g + 1) * P].bitcast(FP8X4),
-                    lhsT_scale=zs[:, ut, g * P : (g + 1) * P],
-                    rhs=cq[:, g, cols].bitcast(FP8X4),
-                    rhs_scale=cs[:, g, cols],
-                    start=(g == 0),
-                    stop=(g == VG - 1),
-                )
+            mx_group(
+                bank[:],
+                lambda g: zq[:, g, units].bitcast(FP8X4),
+                lambda g: zs[:, g, units],
+                lambda g: cq[:, g, cols].bitcast(FP8X4),
+                lambda g: cs[:, g, cols],
+            )
+            staged["m3", oc, ut] = bank
+
+        def y(engine, oc, ut):
+            pair, a = divmod(ut, 2)
             if a == 0:
                 staged["y", oc, pair] = rows_tile(F32, GROUP)
-            nc.vector.tensor_tensor(out=staged["y", oc, pair][:, a, :], in0=bank[:], in1=bias_sb[:, cols], op=ADD)
+            nc.vector.tensor_tensor(
+                out=staged["y", oc, pair][:, a, :],
+                in0=staged["m3", oc, ut][:],
+                in1=bias_sb[:, (oc - FIRST) * GROUP : (oc - FIRST + 1) * GROUP],
+                op=ADD,
+            )
 
-        def store_y(oc, pair, tiles=slice(0, 2)):
+        def mA(engine, oc, half, t):
+            units = slice(half * HALF, (half + 1) * HALF)
+            cols = slice(oc * GROUP + t * P, oc * GROUP + (t + 1) * P)
+            bank = acc_bank()
+            mx_group(
+                bank[:],
+                lambda g: cq[:, g, cols].bitcast(FP8X4),
+                lambda g: cs[:, g, cols],
+                lambda g: zq[:, g, units].bitcast(FP8X4),
+                lambda g: zs[:, g, units],
+            )
+            staged["mA", oc, half, t] = bank
+
+        def aA(engine, oc, half, t):
+            if t == 0:
+                staged["yt", oc, half] = wide_tile(F32, HALF)
+            dst, bank = staged["yt", oc, half][:, t, :], staged["mA", oc, half, t][:]
+            if engine == "S":
+                nc.scalar.activation(out=dst, in_=bank, func=IDENTITY, bias=bias_col[:, t : t + 1], scale=1.0)
+            else:
+                nc.vector.tensor_scalar(out=dst, in0=bank, scalar1=bias_col[:, t : t + 1], scalar2=None, op0=ADD)
+
+        def tb(engine, oc, pair, a):
+            ut = (2 * pair + a) % 4
+            bank = turn_bank()[:].rearrange("p (t m) -> p t m", t=PACK)
+            for t in range(PACK):
+                nc.tensor.transpose(bank[:, t, :], staged["yt", oc, pair // 2][:, t, ut * P : (ut + 1) * P], ident[:])
+            staged["back", oc, pair, a] = bank
+
+        def rb(engine, oc, pair, a):
+            if a == 0:
+                staged["y", oc, pair] = rows_tile(F32, GROUP)
+            move(
+                engine,
+                staged["y", oc, pair][:, a, :].rearrange("p (m t) -> p m t", t=PACK),
+                staged["back", oc, pair, a].rearrange("p t m -> p m t"),
+            )
+
+        def st(engine, oc, pair, tiles=slice(0, 2)):
             rows = out_0[pair * 2 * P : (pair + 1) * 2 * P, oc * GROUP : (oc + 1) * GROUP]
             nc.sync.dma_start(
                 out=rows.rearrange("(a p) o -> p a o", p=P)[:, tiles, :], in_=staged["y", oc, pair][:, tiles, :]
             )
 
-        def round_y(engine, oc, pair, tiles=slice(0, 2)):
+        def cast(engine, oc, pair, tiles=slice(0, 2)):
             if tiles.start == 0:
                 staged["y16", oc, pair] = stage.tile([P, 2, 2 * P, 2], BF16, name="y16", bufs=4)
             units = slice(tiles.start * P, tiles.stop * P)
             src = staged["y", oc, pair][:].rearrange("p a (m h e) -> p h (a m) e", h=2, e=2)
-            interleave(engine, staged["y16", oc, pair][:, :, units, :], src[:, :, units, :])
+            move(engine, staged["y16", oc, pair][:, :, units, :], src[:, :, units, :])
 
-        def turn_y(oc, pair, tiles=slice(0, 2)):
+        def ty(engine, oc, pair, tiles=slice(0, 2)):
             words = staged["y16", oc, pair][:].rearrange("p h n e -> p h (n e)").bitcast(F32)
             bank = turn_bank()[:].rearrange("p (h u) -> p h u", h=2)
             for a in range(tiles.start, tiles.stop):
@@ -271,199 +440,46 @@ def tile_structural_model_counterfactual_k1_kernel(
                     nc.tensor.transpose(bank[:, h, a * P : (a + 1) * P], words[:, h, a * P : (a + 1) * P], ident[:])
             staged["yb", oc, pair, tiles.start] = bank
 
-        def group_y(oc, pair, tiles=slice(0, 2)):
-            if tiles.start == 0:
-                staged["yg", oc, pair] = stage.tile([P, PIECE * PACK], BF16, name="yg", bufs=4, align_bytes=64)
+        def gy(engine, oc, pair, tiles=slice(0, 2)):
+            if pair % 2 == 0:
+                staged["yg", oc, pair // 2] = piece_tile("S")
             units = slice(tiles.start * P, tiles.stop * P)
-            nc.scalar.copy(
-                out=staged["yg", oc, pair][:].bitcast(F32).rearrange("p (u h) -> p u h", h=2)[:, units, :],
-                in_=staged["yb", oc, pair, tiles.start].rearrange("p h u -> p u h")[:, units, :],
+            part = staged["yg", oc, pair // 2][:, (pair % 2) * PIECE * PACK : (pair % 2 + 1) * PIECE * PACK]
+            move(
+                engine,
+                part.bitcast(F32).rearrange("p (u h) -> p u h", h=2)[:, units, :],
+                staged["yb", oc, pair, tiles.start].rearrange("p h u -> p u h")[:, units, :],
             )
 
-        def quantize_y(oc, pair, tiles=slice(0, 2)):
-            units = slice(pair * PIECE + tiles.start * P, pair * PIECE + tiles.stop * P)
-            values = staged["yg", oc, pair][:, tiles.start * GROUP : tiles.stop * GROUP]
+        def qy(engine, oc, first, count):
+            units = slice(first * P, (first + count) * P)
+            values = staged["yg", oc, first // 4][:, (first % 4) * GROUP : (first % 4 + count) * GROUP]
             quantize(yq[:, oc, units], ys[:, oc, units], values)
 
-        def store_words(oc, first, last):
-            units = slice(first * PIECE, (last + 1) * PIECE)
+        def sw(engine, oc, first, count):
+            units = slice(first * PIECE, (first + count) * PIECE)
             nc.sync.dma_start(
                 out=out_1[oc].rearrange("p m t -> p (m t)").bitcast(I32)[:, units],
                 in_=yq[:, oc, units].bitcast(I32),
             )
 
-        def store_scales(queues, groups):
+        def ss(engine, last):
+            groups = slice(2, 3) if last else slice(0, 2)
             for q in range(4):
-                queues[q % len(queues)].dma_start(
+                nc.sync.dma_start(
                     out=out_2[groups, 4 * q : 4 * q + 4, :].rearrange("g r n -> r g n").bitcast(I32),
                     in_=ys[32 * q : 32 * q + 4, groups, :].bitcast(I32),
                 )
 
-        S, G, V = "scalar", "gpsimd", "vector"
-        order_b_codes(0, 0)
-        order_b_codes(1, 0)
-        order_b_scales(0)
-        order_b_scales(1)
-        for pair in range(3):
-            for g in range(VG):
-                turn_x(pair, g)
-        quantize_x(0, 0)
-        quantize_x(0, 1)
-        order_b_codes(0, 1)
-        order_b_codes(1, 1)
-        noise(0, 0, 0)
-        noise(0, 0, 1)
-        for g in range(VG):
-            turn_x(3, g)
-        lay(G, ("r", 0, 0))
-        noise(0, 0, 2)
-        noise(0, 0, 3)
-        lay(S, ("r", 0, 1))
-        lay(S, ("e", 0, 0))
-        lay(S, ("e", 0, 1))
-        quantize_x(1, 0)
-        quantize_x(1, 1)
-        quantize_piece(("r", 0, 0))
-        lay(G, ("r", 0, 2))
-        noise(0, 1, 0)
-        noise(0, 1, 1)
-        noise(0, 1, 2)
-        quantize_piece(("r", 0, 1))
-        quantize_piece(("r", 0, 2))
-        lay(G, ("r", 1, 0))
-        noise(0, 1, 3)
-        lay(S, ("e", 1, 0))
-        lay(S, ("e", 1, 1))
-        noise(1, 0, 0)
-        noise(1, 0, 1)
-        quantize_piece(("e", 0, 0))
-        quantize_piece(("e", 0, 1))
-        quantize_piece(("r", 1, 0))
-        lay(G, ("r", 1, 1))
-        lay(S, ("r", 0, 3))
-        noise(1, 0, 2)
-        noise(1, 0, 3)
-        lay(S, ("r", 1, 2))
-        lay(S, ("e", 0, 2))
-        noise(1, 1, 0)
-        quantize_piece(("e", 1, 0))
-        quantize_piece(("e", 1, 1))
-        quantize_piece(("r", 1, 1))
-        lay(G, ("r", 1, 3))
-        noise(1, 1, 1)
-        noise(1, 1, 2)
-        noise(1, 1, 3)
-        quantize_piece(("r", 0, 3))
-        quantize_piece(("r", 1, 2))
-        quantize_piece(("r", 1, 3))
-        lay(G, ("c", 0, 0))
-        lay(S, ("e", 1, 2))
-        lay(S, ("e", 0, 3))
-        lay(S, ("e", 1, 3))
-        counterfactual(0, 0)
-        counterfactual(1, 0)
-        counterfactual(2, 0)
-        quantize_piece(("e", 0, 2))
-        quantize_piece(("e", 1, 2))
-        quantize_piece(("c", 0, 0))
-        lay(G, ("c", 1, 0))
-        lay(S, ("c", 0, 1))
-        lay(S, ("c", 1, 1))
-        counterfactual(0, 1)
-        counterfactual(1, 1)
-        counterfactual(2, 1)
-        quantize_piece(("e", 0, 3))
-        quantize_piece(("e", 1, 3))
-        quantize_z(0)
-        quantize_z(1)
-        quantize_piece(("c", 1, 0))
-        lay(G, ("c", 0, 2))
-        lay(S, ("c", 1, 2))
-        counterfactual(3, 0)
-        counterfactual(3, 1)
-        counterfactual(4, 0)
-        quantize_piece(("c", 0, 1))
-        quantize_piece(("c", 1, 1))
-        quantize_z(2)
-        quantize_z(3)
-        quantize_piece(("c", 0, 2))
-
-        units = [(oc, pair) for oc, half in ((0, 0), (1, 0), (0, 1), (1, 1), (2, 0), (2, 1)) for pair in (2 * half, 2 * half + 1)]
-        late = [("c", 0, 3), ("c", 0, 4), ("c", 1, 4), ("c", 0, 5), ("c", 1, 5)]
-
-        def outcomes(n):
-            oc, pair = units[n]
-            outcome(oc, 2 * pair)
-            outcome(oc, 2 * pair + 1)
-            store_y(oc, pair)
-
-        done = set()
-
-        def finish(n):
-            oc, pair = units[n]
-            quantize_y(oc, pair)
-            done.add(n)
-            if n ^ 1 in done:
-                store_words(oc, pair & 2, pair | 1)
-
-        def turn_and_group(n):
-            turn_y(*units[n])
-            group_y(*units[n])
-
-        lay(S, ("c", 1, 3))
-        for n in range(4):
-            lay(G, late[n])
-            counterfactual(4 + n, 1)
-            if n < 3:
-                counterfactual(5 + n, 0)
-            outcomes(n)
-            if n >= 2:
-                turn_and_group(n - 2)
-            round_y(S, *units[n])
-            if n == 0:
-                quantize_piece(("c", 1, 2))
-            if n == 1:
-                quantize_piece(("c", 1, 3))
-            if n >= 3:
-                finish(n - 3)
-            quantize_z(4 + n)
-            quantize_piece(late[n])
-        lay(G, late[4])
-        for n in range(4, 10, 2):
-            outcomes(n)
-            round_y(S, *units[n])
-            outcomes(n + 1)
-            turn_and_group(n - 2)
-            turn_and_group(n - 1)
-            round_y(S, *units[n + 1])
-            finish(n - 3)
-            if n > 4:
-                finish(n - 4)
-            if n == 4:
-                quantize_piece(late[4])
-        outcomes(10)
-        turn_and_group(8)
-        finish(6)
-        finish(7)
-        store_scales([nc.sync], slice(0, 2))
-        round_y(V, *units[10])
-        oc, pair = units[11]
-        outcome(oc, 2 * pair)
-        outcome(oc, 2 * pair + 1)
-        turn_and_group(9)
-        for a in range(2):
-            tiles = slice(a, a + 1)
-            store_y(oc, pair, tiles)
-            round_y(V, oc, pair, tiles)
-        turn_and_group(10)
-        finish(8)
-        finish(9)
-        for a in range(2):
-            tiles = slice(a, a + 1)
-            turn_y(oc, pair, tiles)
-            group_y(oc, pair, tiles)
-        quantize_y(*units[10])
-        for a in range(2):
-            quantize_y(oc, pair, slice(a, a + 1))
-        store_words(oc, pair - 1, pair)
-        store_scales([nc.scalar, nc.sync], slice(2, 3))
+        steps = {
+            "pc": pc, "ps": ps, "tx": tx, "xo": xo, "qx": qx, "me": me, "ee": ee, "m1": m1, "e1": e1, "lay": lay,
+            "qp": qp, "m2": m2, "z": z, "qz": qz, "m3": m3, "y": y, "mA": mA, "aA": aA, "tb": tb, "rb": rb,
+            "st": st, "cast": cast, "ty": ty, "gy": gy, "qy": qy, "sw": sw, "ss": ss,
+            "st1": lambda e, a: st(e, 2, 3, slice(a, a + 1)),
+            "cast1": lambda e, a: cast(e, 2, 3, slice(a, a + 1)),
+            "ty1": lambda e, a: ty(e, 2, 3, slice(a, a + 1)),
+            "gy1": lambda e, a: gy(e, 2, 3, slice(a, a + 1)),
+            "qy1": lambda e, a: qy(e, 2, 6 + a, 1),
+        }
+        for step in ORDER:
+            steps[step[0]](*step[1:])

@@ -16,87 +16,14 @@ FP4X4 = mybir.dt.float4_e2m1fn_x4
 ADD = mybir.AluOpType.add
 SUB = mybir.AluOpType.subtract
 MULT = mybir.AluOpType.mult
-IDENTITY = mybir.ActivationFunctionType.Identity
 
 P = 128
-PACK = 4
-GROUP = P * PACK
-VG = VARS // GROUP
-OG = OUTS // GROUP
-UT = UNITS // P
-HALF = 512
-PIECE = 256
-TURNED = (0,)
-FIRST = 1
-ORDER = [
-    ("tx", "P", 0, 1), ("xo", "S", 0, 1), ("pc", "V", 0, 0), ("pc", "V", 1, 0),
-    ("tx", "P", 0, 0), ("ps", "V", 0), ("tx", "P", 1, 0), ("xo", "S", 0, 0),
-    ("ps", "V", 1), ("qx", "V", 1, 0, 1), ("tx", "P", 1, 1), ("qx", "V", 0, 0, 1),
-    ("me", "P", 0, 0, 2), ("lay", "G", "r", 0, 3, 1), ("xo", "S", 1, 0), ("xo", "S", 1, 1),
-    ("me", "P", 0, 0, 0), ("pc", "V", 0, 1), ("lay", "S", "r", 0, 1, 1), ("qx", "V", 0, 1, 1),
-    ("qx", "V", 1, 1, 1), ("pc", "V", 1, 1), ("me", "P", 1, 0, 2), ("lay", "S", "r", 0, 0, 1),
-    ("tx", "P", 2, 0), ("ee", "V", 0, 0, 2), ("ee", "V", 0, 0, 0), ("ee", "V", 1, 0, 2),
-    ("qp", "V", "r", 0, 3), ("tx", "P", 3, 0), ("xo", "S", 2, 0), ("me", "P", 0, 1, 2),
-    ("lay", "V", "e", 0, 0, 1), ("tx", "P", 2, 1), ("tx", "P", 3, 1), ("me", "P", 0, 1, 0),
-    ("qp", "V", "r", 0, 0), ("ee", "V", 0, 1, 2), ("lay", "S", "r", 0, 2, 1), ("me", "P", 1, 0, 0),
-    ("xo", "S", 3, 0), ("qp", "V", "r", 0, 1), ("qp", "V", "r", 0, 2), ("qp", "V", "e", 0, 0),
-    ("qx", "V", 0, 2, 2), ("xo", "S", 2, 1), ("xo", "S", 3, 1), ("ee", "V", 0, 1, 0),
-    ("qx", "V", 1, 2, 2), ("me", "P", 1, 1, 0), ("lay", "S", "r", 1, 0, 2), ("me", "P", 1, 1, 2),
-    ("ee", "V", 1, 0, 0), ("m1", "P", 1, 1, 3), ("ee", "V", 1, 1, 0), ("m1", "P", 1, 1, 1),
-    ("lay", "S", "r", 1, 2, 2), ("m1", "P", 1, 1, 2), ("ee", "V", 1, 1, 2), ("lay", "S", "e", 1, 1, 1),
-    ("qp", "V", "r", 1, 0), ("lay", "G", "e", 1, 0, 1), ("lay", "S", "c", 1, 0, 2), ("qp", "V", "e", 1, 0),
-    ("m1", "P", 1, 1, 0), ("lay", "G", "e", 0, 1, 1), ("e1", "V", 1, 1, 3), ("m1", "P", 1, 0, 3),
-    ("e1", "V", 1, 1, 1), ("e1", "V", 1, 1, 2), ("e1", "V", 1, 1, 0), ("m1", "P", 1, 0, 2),
-    ("qp", "V", "r", 1, 2), ("m1", "P", 1, 0, 0), ("qp", "V", "e", 0, 1), ("m1", "P", 1, 0, 1),
-    ("qp", "V", "e", 1, 1), ("m2", "P", 0, 1), ("lay", "S", "e", 1, 2, 2), ("e1", "V", 1, 0, 3),
-    ("e1", "V", 1, 0, 2), ("e1", "V", 1, 0, 0), ("m2", "P", 3, 1), ("m2", "P", 1, 1),
-    ("m2", "P", 0, 0), ("z", "V", 0, 1), ("lay", "G", "c", 0, 0, 1), ("e1", "V", 1, 0, 1),
-    ("m2", "P", 2, 1), ("m2", "P", 3, 0), ("z", "V", 3, 1), ("z", "V", 1, 1),
-    ("z", "V", 0, 0), ("qz", "V", 1, 0, 1), ("z", "V", 2, 1), ("lay", "S", "e", 0, 2, 2),
-    ("qp", "V", "e", 1, 2), ("qp", "V", "c", 1, 0), ("m2", "P", 1, 0), ("qp", "V", "e", 0, 2),
-    ("m2", "P", 2, 0), ("m2", "P", 4, 1), ("qp", "V", "c", 0, 0), ("z", "V", 3, 0),
-    ("lay", "G", "c", 0, 2, 1), ("m2", "P", 5, 1), ("z", "V", 1, 0), ("z", "V", 4, 1),
-    ("m2", "P", 7, 1), ("z", "V", 2, 0), ("m2", "P", 4, 0), ("qz", "V", 1, 1, 1),
-    ("qz", "V", 0, 0, 1), ("qz", "V", 0, 1, 1), ("z", "V", 5, 1), ("lay", "S", "c", 0, 1, 1),
-    ("m2", "P", 6, 0), ("mA", "P", 0, 0, 0), ("z", "V", 7, 1), ("lay", "S", "c", 1, 2, 2),
-    ("mA", "P", 0, 0, 1), ("lay", "S", "c", 1, 4, 2), ("m2", "P", 6, 1), ("z", "V", 4, 0),
-    ("qp", "V", "c", 0, 1), ("m2", "P", 5, 0), ("aA", "S", 0, 0, 0), ("z", "V", 6, 0),
-    ("mA", "P", 0, 0, 3), ("lay", "S", "c", 0, 3, 1), ("qp", "V", "c", 1, 2), ("z", "V", 6, 1),
-    ("mA", "P", 0, 0, 2), ("aA", "S", 0, 0, 1), ("qp", "V", "c", 0, 3), ("aA", "S", 0, 0, 3),
-    ("aA", "S", 0, 0, 2), ("lay", "S", "c", 0, 4, 1), ("qp", "V", "c", 0, 2), ("qz", "V", 1, 2, 2),
-    ("z", "V", 5, 0), ("m2", "P", 7, 0), ("z", "V", 7, 0), ("m3", "P", 1, 2),
-    ("tb", "P", 0, 0, 0), ("tb", "P", 0, 0, 1), ("lay", "G", "c", 0, 5, 1), ("m3", "P", 1, 0),
-    ("rb", "S", 0, 0, 0), ("y", "V", 1, 2), ("m3", "P", 1, 3), ("rb", "S", 0, 0, 1),
-    ("m3", "P", 1, 1), ("qz", "V", 0, 2, 2), ("lay", "S", "y", 0, 1, 1), ("m3", "P", 1, 4),
-    ("qp", "V", "c", 0, 5), ("qp", "V", "c", 0, 4), ("y", "V", 1, 3), ("mA", "P", 0, 1, 0),
-    ("st", "D", 0, 0), ("y", "V", 1, 0), ("tb", "P", 0, 1, 0), ("tb", "P", 0, 1, 1),
-    ("m3", "P", 1, 5), ("y", "V", 1, 4), ("y", "V", 1, 1), ("cast", "S", 1, 1),
-    ("qp", "V", "c", 1, 4), ("mA", "P", 0, 1, 3), ("aA", "S", 0, 1, 0), ("mA", "P", 0, 1, 2),
-    ("lay", "G", "y", 0, 0, 1), ("m3", "P", 2, 0), ("rb", "S", 0, 1, 0), ("rb", "S", 0, 1, 1),
-    ("st", "D", 1, 1), ("m3", "P", 2, 1), ("cast", "G", 1, 0), ("aA", "S", 0, 1, 2),
-    ("y", "V", 1, 5), ("st", "D", 1, 0), ("m3", "P", 2, 4), ("aA", "V", 0, 1, 3),
-    ("cast", "S", 1, 2), ("y", "V", 2, 0), ("st", "D", 1, 2), ("mA", "P", 0, 1, 1),
-    ("aA", "S", 0, 1, 1), ("qp", "V", "y", 0, 1), ("m3", "P", 2, 5), ("y", "V", 2, 1),
-    ("m3", "P", 1, 6), ("y", "V", 2, 4), ("cast", "S", 2, 0), ("m3", "P", 1, 7),
-    ("m3", "P", 2, 2), ("qp", "V", "y", 0, 0), ("st", "D", 0, 1), ("ty", "P", 1, 0),
-    ("lay", "S", "y", 0, 3, 1), ("m3", "P", 2, 3), ("tb", "P", 0, 2, 0), ("y", "V", 2, 5),
-    ("y", "V", 1, 6), ("y", "V", 1, 7), ("st", "D", 2, 0), ("ty", "P", 1, 1),
-    ("y", "V", 2, 2), ("sw", "D", 0, 0, 2), ("gy", "S", 1, 0), ("rb", "S", 0, 2, 0),
-    ("lay", "G", "y", 0, 2, 1), ("tb", "P", 0, 2, 1), ("qp", "V", "y", 0, 2), ("gy", "S", 1, 1),
-    ("qp", "V", "y", 0, 3), ("y", "V", 2, 3), ("m3", "P", 2, 6), ("cast", "V", 1, 3),
-    ("cast", "S", 2, 2), ("st", "D", 2, 2), ("ty", "P", 1, 2), ("ty", "P", 1, 3),
-    ("st", "D", 1, 3), ("gy", "S", 1, 2), ("rb", "V", 0, 2, 1), ("gy", "S", 1, 3),
-    ("ty", "P", 2, 0), ("m3", "P", 2, 7), ("tb", "P", 0, 3, 0), ("tb", "P", 0, 3, 1),
-    ("sw", "D", 0, 2, 2), ("qy", "V", 1, 0, 4), ("rb", "S", 0, 3, 0), ("y", "V", 2, 6),
-    ("gy", "V", 2, 0), ("rb", "S", 0, 3, 1), ("y", "V", 2, 7), ("st", "D", 2, 1),
-    ("st", "D", 0, 2), ("st1", "D", 0), ("cast", "G", 2, 1), ("qy", "V", 1, 4, 4),
-    ("cast1", "V", 0), ("sw", "D", 1, 0, 2), ("ty", "P", 2, 1), ("gy", "V", 2, 1),
-    ("cast1", "V", 1), ("st1", "D", 1), ("sw", "D", 1, 2, 2), ("ty", "P", 2, 2),
-    ("ss", "D", 0), ("qy", "V", 2, 0, 4), ("gy", "S", 2, 2), ("ty1", "P", 0),
-    ("st", "D", 0, 3), ("ty1", "P", 1), ("qy", "V", 2, 4, 2), ("gy1", "S", 0),
-    ("qy1", "V", 0), ("gy1", "S", 1), ("qy1", "V", 1), ("sw", "D", 2, 0, 2),
-    ("sw", "D", 2, 2, 1), ("ss", "D", 1), ("sw", "D", 2, 3, 1),
-]
+SLOTS = 4
+GROUP = P * SLOTS
+VAR_GROUPS = VARS // GROUP
+OUT_GROUPS = OUTS // GROUP
+QUARTER = 2 * P
+HALF = 2 * QUARTER
 
 
 def tile_structural_model_counterfactual_k1_kernel(
@@ -105,381 +32,370 @@ def tile_structural_model_counterfactual_k1_kernel(
     nc = tc.nc
     with ExitStack() as ctx:
         keep = ctx.enter_context(tc.tile_pool(name="keep", bufs=1))
-        stage = ctx.enter_context(tc.tile_pool(name="stage", bufs=3))
+        stage = ctx.enter_context(tc.tile_pool(name="stage", bufs=1))
         psum = ctx.enter_context(tc.psum_pool(name="psum", bufs=1))
         ctx.enter_context(tc.manual_schedule())
 
         def kept(name, shape, dtype):
             return keep.tile(shape, dtype, name=name, align_bytes=64)
 
-        ident = kept("ident", [P, P], F32)
-        b_raw = kept("b_raw", [P, VG, VG, 2 * GROUP], U8)
-        b_codes = kept("b_codes", [P, VG, 2 * VARS], U8)
-        bs_raw = kept("bs_raw", [P, VG, VARS], U8)
-        b_sc = kept("b_sc", [P, VG, VARS], U8)
-        shift_sb = kept("shift_sb", [P, VG, PACK], BF16)
-        bias_col = kept("bias_col", [P, PACK], BF16)
-        bias_sb = kept("bias_sb", [P, OUTS - GROUP], BF16)
-        c_raw = kept("c_raw", [P, VG, PACK, OUTS], BF16)
-        xg = kept("xg", [P, VG, UNITS, PACK], BF16)
-        e32 = kept("e32", [P, VG, PACK, UNITS], F32)
-        xq = kept("xq", [P, VG, UNITS], U32)
-        xs = kept("xs", [P, VG, UNITS], U8)
-        eq = kept("eq", [P, VG, UNITS], U32)
-        es = kept("es", [P, VG, UNITS], U8)
-        zq = kept("zq", [P, VG, UNITS], U32)
-        zs = kept("zs", [P, VG, UNITS], U8)
-        rq = kept("rq", [P, VG, VARS], U32)
-        rs = kept("rs", [P, VG, VARS], U8)
-        cq = kept("cq", [P, VG, OUTS], U32)
-        cs = kept("cs", [P, VG, OUTS], U8)
-        yq = kept("yq", [P, OG, UNITS], U32)
-        ys = kept("ys", [P, OG, UNITS], U8)
+        def planes(name, groups, width):
+            return kept(name + "_codes", [P, groups, width], U32), kept(name + "_scales", [P, groups, width], U8)
 
-        def acc_bank():
-            return psum.tile([P, GROUP], F32, name="acc", bufs=5)
+        ident = kept("ident", [P, P], F32)
+        b_raw = kept("b_raw", [P, VAR_GROUPS, VAR_GROUPS, 2 * GROUP], U8)
+        b_codes = kept("b_codes", [P, VAR_GROUPS, 2 * VARS], U8)
+        b_scales_raw = kept("b_scales_raw", [P, VAR_GROUPS, VARS], U8)
+        b_scales_sb = kept("b_scales_sb", [P, VAR_GROUPS, VARS], U8)
+        shift_sb = kept("shift_sb", [P, VAR_GROUPS, SLOTS], BF16)
+        bias_sb = kept("bias_sb", [P, OUTS], BF16)
+        r_raw = kept("r_raw", [P, VAR_GROUPS, SLOTS, VARS], BF16)
+        c_raw = kept("c_raw", [P, VAR_GROUPS, SLOTS, OUTS], BF16)
+        x_t = kept("x_t", [P, VAR_GROUPS, UNITS, SLOTS], BF16)
+        e_t = kept("e_t", [P, VAR_GROUPS, SLOTS, UNITS], F32)
+        mx = {
+            "x": planes("x", VAR_GROUPS, UNITS),
+            "e": planes("e", VAR_GROUPS, UNITS),
+            "z": planes("z", VAR_GROUPS, UNITS),
+            "r": planes("r", VAR_GROUPS, VARS),
+            "c": planes("c", VAR_GROUPS, OUTS),
+            "y": planes("y", OUT_GROUPS, UNITS),
+        }
+
+        def sum_bank():
+            return psum.tile([P, GROUP], F32, name="sum_bank", bufs=5)
 
         def turn_bank():
-            return psum.tile([P, GROUP], F32, name="turn", bufs=3)
-
-        def quantize(codes, scales, values):
-            nc.vector.quantize_mx(out=codes.bitcast(FP8X4), scales=scales, in_=values)
-
-        nc.vector.memset(bs_raw[:].rearrange("p g n -> p (g n)").bitcast(I32), 0)
-        make_identity(nc, ident[:])
-
-        def load_b(go):
-            cols = slice(go * 2 * GROUP, (go + 1) * 2 * GROUP)
-            nc.sync.dma_start(
-                out=b_raw[:, go].bitcast(I32),
-                in_=b_words[:, :, cols].rearrange("g p n -> p g n").bitcast(I32),
-            )
+            return psum.tile([P, 2, QUARTER], F32, name="turn_bank", bufs=3)
 
         def rows_tile(dtype, width):
             return stage.tile([P, 2, width], dtype, name="rows", bufs=4)
 
+        def piece_tile(engine):
+            if engine == "gpsimd":
+                return stage.tile([P, QUARTER * SLOTS], BF16, name="gpsimd_piece", bufs=1, align_bytes=64)
+            return stage.tile([P, HALF * SLOTS], BF16, name="piece", bufs=5, align_bytes=64)
+
+        def span(first, count, width):
+            return slice(first * width, (first + count) * width)
+
+        nc.vector.memset(b_scales_raw[:].rearrange("p g n -> p (g n)").bitcast(I32), 0)
+        make_identity(nc, ident[:])
+
+        def load_b(go):
+            nc.sync.dma_start(
+                out=b_raw[:, go].bitcast(I32),
+                in_=b_words[:, :, span(go, 1, 2 * GROUP)].rearrange("g p n -> p g n").bitcast(I32),
+            )
+
         x_rows = x.rearrange("(i p) k -> p i k", p=P)
-        x_raw = [rows_tile(BF16, VARS) for pair in range(UT // 2)]
+        x_raw = [rows_tile(BF16, VARS) for quarter in range(4)]
         load_b(0)
         nc.sync.dma_start(out=x_raw[0][:], in_=x_rows[:, 0:2, :])
         for q in range(4):
             nc.sync.dma_start(
-                out=bs_raw[32 * q : 32 * q + 4, :, :].bitcast(I32),
-                in_=b_scales[:, 4 * q : 4 * q + 4, :].rearrange("g r n -> r g n").bitcast(I32),
+                out=b_scales_raw[32 * q : 32 * q + 4, :, :].bitcast(I32),
+                in_=b_scales[:, 4 * q : 4 * q + 4, :].rearrange("g j n -> j g n").bitcast(I32),
             )
-        for i in range(2, 4):
-            nc.sync.dma_start(out=x_raw[1][:, i % 2, :], in_=x_rows[:, i, :])
-        nc.sync.dma_start(out=shift_sb[:], in_=shift.rearrange("(g p t) -> p g t", p=P, t=PACK))
+        for a in range(2):
+            nc.sync.dma_start(out=x_raw[1][:, a, :], in_=x_rows[:, 2 + a, :])
+        nc.sync.dma_start(out=shift_sb[:], in_=shift.rearrange("(g p t) -> p g t", p=P, t=SLOTS))
+        for quarter in range(2, 4):
+            nc.sync.dma_start(out=x_raw[quarter][:], in_=x_rows[:, span(quarter, 1, 2), :])
         load_b(1)
-
-        def wide_tile(dtype, width):
-            return stage.tile([P, PACK, width], dtype, name="wide", bufs=2)
-
-        r_raw = [wide_tile(BF16, VARS) for g in range(VG)]
-        for g in range(VG):
-            rows = slice(g * GROUP, (g + 1) * GROUP)
-            nc.sync.dma_start(out=r_raw[g][:], in_=r[rows, :].rearrange("(p j) n -> p j n", j=PACK))
-            if g == 0:
-                nc.sync.dma_start(out=x_raw[2][:], in_=x_rows[:, 4:6, :])
-                nc.sync.dma_start(out=x_raw[3][:], in_=x_rows[:, 6:8, :])
-        for g in range(VG):
-            rows = slice(g * GROUP, (g + 1) * GROUP)
-            nc.sync.dma_start(out=c_raw[:, g], in_=c[rows, :].rearrange("(p j) n -> p j n", j=PACK))
-        nc.sync.dma_start(out=bias_col[:], in_=bias[0:GROUP].rearrange("(p t) -> p t", t=PACK))
-        nc.sync.dma_start(out=bias_sb[:], in_=bias[GROUP:OUTS].partition_broadcast(P))
+        for raw, weight in ((r_raw, r), (c_raw, c)):
+            for g in range(VAR_GROUPS):
+                nc.sync.dma_start(
+                    out=raw[:, g], in_=weight[span(g, 1, GROUP), :].rearrange("(p t) n -> p t n", t=SLOTS)
+                )
+        nc.sync.dma_start(out=bias_sb[:], in_=bias.partition_broadcast(P))
 
         staged = {}
 
         def move(engine, dst, src):
-            if engine == "S":
+            if engine == "scalar":
                 nc.scalar.copy(out=dst, in_=src)
-            elif engine == "V":
+            elif engine == "vector":
                 nc.vector.tensor_copy(out=dst, in_=src)
             else:
                 nc.gpsimd.tensor_scalar(out=dst, in0=src, scalar1=1.0, scalar2=0.0, op0=MULT, op1=ADD)
 
-        def piece_tile(engine):
-            if engine == "G":
-                return stage.tile([P, PIECE * PACK], BF16, name="piece_gpsimd", bufs=1, align_bytes=64)
-            return stage.tile([P, 2 * PIECE * PACK], BF16, name="piece", bufs=5, align_bytes=64)
+        def quantize(name, g, cols, values):
+            codes, scales = mx[name]
+            nc.vector.quantize_mx(out=codes[:, g, cols].bitcast(FP8X4), scales=scales[:, g, cols], in_=values)
 
-        def mx_group(out, lhsT, lhsT_scale, rhs, rhs_scale):
-            for g in range(VG):
+        def operand(name, g, cols):
+            if name == "b":
+                return b_codes[:, g, 2 * cols.start : 2 * cols.stop].bitcast(FP4X4), b_scales_sb[:, g, cols]
+            codes, scales = mx[name]
+            return codes[:, g, cols].bitcast(FP8X4), scales[:, g, cols]
+
+        def product(out, stationary, stationary_cols, moving, moving_cols):
+            for g in range(VAR_GROUPS):
+                lhs_codes, lhs_scales = operand(stationary, g, stationary_cols)
+                rhs_codes, rhs_scales = operand(moving, g, moving_cols)
                 nc.tensor.matmul_mx(
                     out=out,
-                    lhsT=lhsT(g),
-                    lhsT_scale=lhsT_scale(g),
-                    rhs=rhs(g),
-                    rhs_scale=rhs_scale(g),
+                    lhsT=lhs_codes,
+                    lhsT_scale=lhs_scales,
+                    rhs=rhs_codes,
+                    rhs_scale=rhs_scales,
                     start=(g == 0),
-                    stop=(g == VG - 1),
+                    stop=(g == VAR_GROUPS - 1),
                 )
 
-        def pc(engine, g, go):
-            cols = slice(go * 2 * GROUP, (go + 1) * 2 * GROUP)
+        def order_b_codes(go):
+            for g in range(VAR_GROUPS):
+                nc.vector.tensor_copy(
+                    out=b_codes[:, g, span(go, 1, 2 * GROUP)].rearrange("p (t m e) -> p t m e", t=SLOTS, e=2),
+                    in_=b_raw[:, go, g, :].rearrange("p (m t e) -> p t m e", t=SLOTS, e=2),
+                )
+
+        def order_b_scales(go):
+            cols = span(go, 1, GROUP)
             nc.vector.tensor_copy(
-                out=b_codes[:, g, cols].rearrange("p (t m e) -> p t m e", t=PACK, e=2),
-                in_=b_raw[:, go, g, :].rearrange("p (m t e) -> p t m e", t=PACK, e=2),
+                out=b_scales_sb[:, :, cols].rearrange("p g (t m) -> p g t m", t=SLOTS),
+                in_=b_scales_raw[:, :, cols].rearrange("p g (m t) -> p g t m", t=SLOTS),
             )
 
-        def ps(engine, go):
-            cols = slice(go * GROUP, (go + 1) * GROUP)
-            nc.vector.tensor_copy(
-                out=b_sc[:, :, cols].rearrange("p g (t m) -> p g t m", t=PACK),
-                in_=bs_raw[:, :, cols].rearrange("p g (m t) -> p g t m", t=PACK),
-            )
-
-        def tx(engine, pair, g):
-            bank = turn_bank()[:].rearrange("p (h u) -> p h u", h=2)
-            for a in range(2):
-                words = x_raw[pair][:, a, :].bitcast(F32)
-                for h in range(2):
-                    nc.tensor.transpose(
-                        bank[:, h, a * P : (a + 1) * P], words[:, 256 * g + h : 256 * (g + 1) : 2], ident[:]
-                    )
-            staged["tx", pair, g] = bank
-
-        def xo(engine, pair, g):
-            move(
-                engine,
-                xg[:].bitcast(F32)[:, g, pair * PIECE : (pair + 1) * PIECE, :],
-                staged["tx", pair, g].rearrange("p h u -> p u h"),
-            )
-
-        def qx(engine, g, first, count):
-            units = slice(first * PIECE, (first + count) * PIECE)
-            quantize(xq[:, g, units], xs[:, g, units], xg[:, g, units, :].rearrange("p u t -> p (u t)"))
-
-        def parents(out, go, t, units):
-            col = (go * PACK + t) * P
-            mx_group(
-                out,
-                lambda g: b_codes[:, g, 2 * col : 2 * (col + P)].bitcast(FP4X4),
-                lambda g: b_sc[:, g, col : col + P],
-                lambda g: xq[:, g, units].bitcast(FP8X4),
-                lambda g: xs[:, g, units],
-            )
-
-        def noise_from(bank, go, t, units):
-            nc.vector.scalar_tensor_tensor(
-                out=e32[:, go, t, units],
-                in0=xg[:, go, units, t],
-                scalar=shift_sb[:, go, t : t + 1],
-                in1=bank,
-                op0=ADD,
-                op1=SUB,
-            )
-
-        def me(engine, pair, go, t0):
-            bank = acc_bank()[:].rearrange("p (t u) -> p t u", t=2)
-            for t in range(2):
+        def turn_x(quarter):
+            for g in range(VAR_GROUPS):
+                bank = turn_bank()
                 for a in range(2):
-                    ut = 2 * pair + a
-                    parents(bank[:, t, a * P : (a + 1) * P], go, t0 + t, slice(ut * P, (ut + 1) * P))
-            staged["me", pair, go, t0] = bank
-
-        def ee(engine, pair, go, t0):
-            for t in range(2):
-                noise_from(
-                    staged["me", pair, go, t0][:, t, :], go, t0 + t, slice(pair * PIECE, (pair + 1) * PIECE)
+                    words = x_raw[quarter][:, a, :].bitcast(F32)
+                    for h in range(2):
+                        nc.tensor.transpose(
+                            bank[:, h, span(a, 1, P)], words[:, 256 * g + h : 256 * (g + 1) : 2], ident[:]
+                        )
+                nc.scalar.copy(
+                    out=x_t[:].bitcast(F32)[:, g, span(quarter, 1, QUARTER), :],
+                    in_=bank[:].rearrange("p h u -> p u h"),
                 )
 
-        def m1(engine, half, go, t):
-            bank = acc_bank()
-            parents(bank[:], go, t, slice(half * HALF, (half + 1) * HALF))
-            staged["m1", half, go, t] = bank
+        def quantize_x(half):
+            units = span(half, 1, HALF)
+            for g in range(VAR_GROUPS):
+                quantize("x", g, units, x_t[:, g, units, :].rearrange("p u t -> p (u t)"))
 
-        def e1(engine, half, go, t):
-            noise_from(staged["m1", half, go, t][:], go, t, slice(half * HALF, (half + 1) * HALF))
+        def noise(half, go):
+            units = span(half, 1, HALF)
+            for t in range(SLOTS):
+                bank = sum_bank()
+                product(bank[:], "b", span(go * SLOTS + t, 1, P), "x", units)
+                nc.vector.scalar_tensor_tensor(
+                    out=e_t[:, go, t, units],
+                    in0=x_t[:, go, units, t],
+                    scalar=shift_sb[:, go, t : t + 1],
+                    in1=bank[:],
+                    op0=ADD,
+                    op1=SUB,
+                )
 
-        def lay(engine, kind, g, first, count):
-            cols = slice(first * PIECE, (first + count) * PIECE)
-            tile = piece_tile(engine)[:, : count * PIECE * PACK]
-            if kind in "ey":
-                if kind == "e":
-                    rows = e32[:, g, :, cols]
-                else:
-                    rows = staged["yt", g, first // 2][:, :, (first % 2) * PIECE : (first % 2 + count) * PIECE]
-                if engine == "G":
-                    dst = tile.rearrange("p (u t) -> p u t", t=PACK)
-                    src = rows.rearrange("p t u -> p u t")
-                else:
-                    dst = tile.rearrange("p (u i t) -> p u t i", i=2, t=PACK)
-                    src = rows.rearrange("p t (u i) -> p u t i", i=2)
-            elif kind == "r" or first // 2 in TURNED:
-                raw = r_raw[g] if kind == "r" else c_raw[:, g]
-                group, t0 = first // 2, 2 * (first % 2)
-                dst = tile.rearrange("p (t m j) -> p t m j", m=P, j=PACK)
-                src = raw[:, :, group * GROUP : (group + 1) * GROUP].rearrange("p j (m t) -> p t m j", t=PACK)
-                src = src[:, t0 : t0 + 2 * count]
-            elif engine == "G":
-                dst = tile.rearrange("p (n j) -> p n j", j=PACK)
-                src = c_raw[:, g, :, cols].rearrange("p j n -> p n j")
+        def lay(engine, name, g, first, count):
+            cols = span(first, count, QUARTER)
+            piece = piece_tile(engine)[:, : count * QUARTER * SLOTS]
+            if name == "r":
+                dst = piece.rearrange("p (s m t) -> p m s t", s=SLOTS, t=SLOTS)
+                src = r_raw[:, g, :, cols].rearrange("p t (m s) -> p m s t", s=SLOTS)
             else:
-                dst = tile.rearrange("p (n i j) -> p n j i", i=4, j=PACK)
-                src = c_raw[:, g, :, cols].rearrange("p j (n i) -> p n j i", i=4)
+                rows = e_t[:, g, :, cols] if name == "e" else c_raw[:, g, :, cols]
+                run = 1 if engine == "gpsimd" else 2 if name == "e" else 4
+                dst = piece.rearrange("p (n i t) -> p n t i", i=run, t=SLOTS)
+                src = rows.rearrange("p t (n i) -> p n t i", i=run)
             move(engine, dst, src)
-            staged["piece", kind, g, first] = (tile, cols)
+            staged[name, g, first] = (cols, piece)
 
-        def qp(engine, kind, g, first):
-            tile, cols = staged["piece", kind, g, first]
-            codes, scales = {"e": (eq, es), "r": (rq, rs), "c": (cq, cs), "y": (yq, ys)}[kind]
-            quantize(codes[:, g, cols], scales[:, g, cols], tile)
+        def quantize_pieces(*keys):
+            for name, g, first in keys:
+                quantize(name, g, *staged[name, g, first])
 
-        def m2(engine, ut, go):
-            units = slice(ut * P, (ut + 1) * P)
-            bank = acc_bank()[:].rearrange("p (t u) -> p t u", t=PACK)
-            for t in range(PACK):
-                col = (go * PACK + t) * P
-                mx_group(
-                    bank[:, t, :],
-                    lambda g: rq[:, g, col : col + P].bitcast(FP8X4),
-                    lambda g: rs[:, g, col : col + P],
-                    lambda g: eq[:, g, units].bitcast(FP8X4),
-                    lambda g: es[:, g, units],
+        def counterfactual(go, *tiles):
+            for ut in tiles:
+                units = span(ut, 1, P)
+                half, a = divmod(ut, 4)
+                bank = sum_bank()[:].rearrange("p (t u) -> p t u", t=SLOTS)
+                for t in range(SLOTS):
+                    product(bank[:, t, :], "r", span(go * SLOTS + t, 1, P), "e", units)
+                if a == 0:
+                    staged["z", go, half] = stage.tile([P, 4, GROUP], BF16, name="z_t", bufs=3, align_bytes=64)
+                nc.vector.tensor_tensor(
+                    out=staged["z", go, half][:, a, :].rearrange("p (u i t) -> p u t i", i=2, t=SLOTS),
+                    in0=bank.rearrange("p t (u i) -> p u t i", i=2),
+                    in1=e_t[:, go, :, units].rearrange("p t (u i) -> p u t i", i=2),
+                    op=ADD,
                 )
-            staged["m2", ut, go] = bank
 
-        def z(engine, ut, go):
-            half, a = divmod(ut, 4)
+        def quantize_z(go, first, count):
+            values = staged["z", go, first // 2][:, span(first % 2, count, 2), :]
+            quantize("z", go, span(first, count, QUARTER), values.rearrange("p a n -> p (a n)"))
+
+        BOTH = slice(0, 2)
+
+        def outcome(oc, quarter, a):
+            cols = span(oc, 1, GROUP)
+            bank = sum_bank()
+            product(bank[:], "z", span(2 * quarter + a, 1, P), "c", cols)
             if a == 0:
-                staged["z", half, go] = stage.tile([P, 4, GROUP], BF16, name="zg", bufs=3, align_bytes=64)
-            nc.vector.tensor_tensor(
-                out=staged["z", half, go][:, a, :].rearrange("p (u i t) -> p u t i", i=2, t=PACK),
-                in0=staged["m2", ut, go].rearrange("p t (u i) -> p u t i", i=2),
-                in1=e32[:, go, :, ut * P : (ut + 1) * P].rearrange("p t (u i) -> p u t i", i=2),
-                op=ADD,
-            )
+                staged["y", oc, quarter] = rows_tile(F32, GROUP)
+            nc.vector.tensor_tensor(out=staged["y", oc, quarter][:, a, :], in0=bank[:], in1=bias_sb[:, cols], op=ADD)
 
-        def qz(engine, go, first, count):
-            units = slice(first * PIECE, (first + count) * PIECE)
-            tiles = slice(2 * (first % 2), 2 * (first % 2 + count))
-            values = staged["z", first // 2, go][:, tiles, :].rearrange("p a n -> p (a n)")
-            quantize(zq[:, go, units], zs[:, go, units], values)
+        def store_y(oc, quarter, tiles):
+            rows = out_0[span(quarter, 1, QUARTER), span(oc, 1, GROUP)].rearrange("(a p) o -> p a o", p=P)
+            nc.sync.dma_start(out=rows[:, tiles, :], in_=staged["y", oc, quarter][:, tiles, :])
 
-        def m3(engine, oc, ut):
-            cols = slice(oc * GROUP, (oc + 1) * GROUP)
-            units = slice(ut * P, (ut + 1) * P)
-            bank = acc_bank()
-            mx_group(
-                bank[:],
-                lambda g: zq[:, g, units].bitcast(FP8X4),
-                lambda g: zs[:, g, units],
-                lambda g: cq[:, g, cols].bitcast(FP8X4),
-                lambda g: cs[:, g, cols],
-            )
-            staged["m3", oc, ut] = bank
+        def outcomes(oc, quarter):
+            for a in range(2):
+                outcome(oc, quarter, a)
+            store_y(oc, quarter, BOTH)
 
-        def y(engine, oc, ut):
-            pair, a = divmod(ut, 2)
-            if a == 0:
-                staged["y", oc, pair] = rows_tile(F32, GROUP)
-            nc.vector.tensor_tensor(
-                out=staged["y", oc, pair][:, a, :],
-                in0=staged["m3", oc, ut][:],
-                in1=bias_sb[:, (oc - FIRST) * GROUP : (oc - FIRST + 1) * GROUP],
-                op=ADD,
-            )
-
-        def mA(engine, oc, half, t):
-            units = slice(half * HALF, (half + 1) * HALF)
-            cols = slice(oc * GROUP + t * P, oc * GROUP + (t + 1) * P)
-            bank = acc_bank()
-            mx_group(
-                bank[:],
-                lambda g: cq[:, g, cols].bitcast(FP8X4),
-                lambda g: cs[:, g, cols],
-                lambda g: zq[:, g, units].bitcast(FP8X4),
-                lambda g: zs[:, g, units],
-            )
-            staged["mA", oc, half, t] = bank
-
-        def aA(engine, oc, half, t):
-            if t == 0:
-                staged["yt", oc, half] = wide_tile(F32, HALF)
-            dst, bank = staged["yt", oc, half][:, t, :], staged["mA", oc, half, t][:]
-            if engine == "S":
-                nc.scalar.activation(out=dst, in_=bank, func=IDENTITY, bias=bias_col[:, t : t + 1], scale=1.0)
-            else:
-                nc.vector.tensor_scalar(out=dst, in0=bank, scalar1=bias_col[:, t : t + 1], scalar2=None, op0=ADD)
-
-        def tb(engine, oc, pair, a):
-            ut = (2 * pair + a) % 4
-            bank = turn_bank()[:].rearrange("p (t m) -> p t m", t=PACK)
-            for t in range(PACK):
-                nc.tensor.transpose(bank[:, t, :], staged["yt", oc, pair // 2][:, t, ut * P : (ut + 1) * P], ident[:])
-            staged["back", oc, pair, a] = bank
-
-        def rb(engine, oc, pair, a):
-            if a == 0:
-                staged["y", oc, pair] = rows_tile(F32, GROUP)
-            move(
-                engine,
-                staged["y", oc, pair][:, a, :].rearrange("p (m t) -> p m t", t=PACK),
-                staged["back", oc, pair, a].rearrange("p t m -> p m t"),
-            )
-
-        def st(engine, oc, pair, tiles=slice(0, 2)):
-            rows = out_0[pair * 2 * P : (pair + 1) * 2 * P, oc * GROUP : (oc + 1) * GROUP]
-            nc.sync.dma_start(
-                out=rows.rearrange("(a p) o -> p a o", p=P)[:, tiles, :], in_=staged["y", oc, pair][:, tiles, :]
-            )
-
-        def cast(engine, oc, pair, tiles=slice(0, 2)):
+        def round_y(engine, oc, quarter, tiles=BOTH):
             if tiles.start == 0:
-                staged["y16", oc, pair] = stage.tile([P, 2, 2 * P, 2], BF16, name="y16", bufs=4)
-            units = slice(tiles.start * P, tiles.stop * P)
-            src = staged["y", oc, pair][:].rearrange("p a (m h e) -> p h (a m) e", h=2, e=2)
-            move(engine, staged["y16", oc, pair][:, :, units, :], src[:, :, units, :])
+                staged["y16", oc, quarter] = stage.tile([P, 2, QUARTER, 2], BF16, name="y16", bufs=5)
+            cols = slice(tiles.start * P, tiles.stop * P)
+            src = staged["y", oc, quarter][:].rearrange("p a (m h e) -> p h (a m) e", h=2, e=2)
+            move(engine, staged["y16", oc, quarter][:, :, cols, :], src[:, :, cols, :])
 
-        def ty(engine, oc, pair, tiles=slice(0, 2)):
-            words = staged["y16", oc, pair][:].rearrange("p h n e -> p h (n e)").bitcast(F32)
-            bank = turn_bank()[:].rearrange("p (h u) -> p h u", h=2)
+        def turn_y(oc, quarter, tiles=BOTH):
+            words = staged["y16", oc, quarter][:].rearrange("p h n e -> p h (n e)").bitcast(F32)
+            bank = turn_bank()
             for a in range(tiles.start, tiles.stop):
                 for h in range(2):
-                    nc.tensor.transpose(bank[:, h, a * P : (a + 1) * P], words[:, h, a * P : (a + 1) * P], ident[:])
-            staged["yb", oc, pair, tiles.start] = bank
-
-        def gy(engine, oc, pair, tiles=slice(0, 2)):
-            if pair % 2 == 0:
-                staged["yg", oc, pair // 2] = piece_tile("S")
+                    nc.tensor.transpose(bank[:, h, span(a, 1, P)], words[:, h, span(a, 1, P)], ident[:])
+            if quarter % 2 == 0:
+                staged["y_t", oc, quarter // 2] = piece_tile("scalar")
             units = slice(tiles.start * P, tiles.stop * P)
-            part = staged["yg", oc, pair // 2][:, (pair % 2) * PIECE * PACK : (pair % 2 + 1) * PIECE * PACK]
-            move(
-                engine,
-                part.bitcast(F32).rearrange("p (u h) -> p u h", h=2)[:, units, :],
-                staged["yb", oc, pair, tiles.start].rearrange("p h u -> p u h")[:, units, :],
+            part = staged["y_t", oc, quarter // 2][:, span(quarter % 2, 1, QUARTER * SLOTS)]
+            nc.scalar.copy(
+                out=part.bitcast(F32).rearrange("p (u h) -> p u h", h=2)[:, units, :],
+                in_=bank[:].rearrange("p h u -> p u h")[:, units, :],
             )
 
-        def qy(engine, oc, first, count):
-            units = slice(first * P, (first + count) * P)
-            values = staged["yg", oc, first // 4][:, (first % 4) * GROUP : (first % 4 + count) * GROUP]
-            quantize(yq[:, oc, units], ys[:, oc, units], values)
+        def quantize_y(oc, first, count):
+            quantize("y", oc, span(first, count, P), staged["y_t", oc, first // 4][:, span(first % 4, count, GROUP)])
 
-        def sw(engine, oc, first, count):
-            units = slice(first * PIECE, (first + count) * PIECE)
+        def store_words(oc, first, count):
+            units = span(first, count, QUARTER)
             nc.sync.dma_start(
                 out=out_1[oc].rearrange("p m t -> p (m t)").bitcast(I32)[:, units],
-                in_=yq[:, oc, units].bitcast(I32),
+                in_=mx["y"][0][:, oc, units].bitcast(I32),
             )
 
-        def ss(engine, last):
-            groups = slice(2, 3) if last else slice(0, 2)
+        def finish_half(oc, half):
+            quantize_y(oc, 4 * half, 4)
+            store_words(oc, 2 * half, 2)
+
+        def store_scales(groups, queues):
             for q in range(4):
-                nc.sync.dma_start(
-                    out=out_2[groups, 4 * q : 4 * q + 4, :].rearrange("g r n -> r g n").bitcast(I32),
-                    in_=ys[32 * q : 32 * q + 4, groups, :].bitcast(I32),
+                queues[q % len(queues)].dma_start(
+                    out=out_2[groups, 4 * q : 4 * q + 4, :].rearrange("g j n -> j g n").bitcast(I32),
+                    in_=mx["y"][1][32 * q : 32 * q + 4, groups, :].bitcast(I32),
                 )
 
-        steps = {
-            "pc": pc, "ps": ps, "tx": tx, "xo": xo, "qx": qx, "me": me, "ee": ee, "m1": m1, "e1": e1, "lay": lay,
-            "qp": qp, "m2": m2, "z": z, "qz": qz, "m3": m3, "y": y, "mA": mA, "aA": aA, "tb": tb, "rb": rb,
-            "st": st, "cast": cast, "ty": ty, "gy": gy, "qy": qy, "sw": sw, "ss": ss,
-            "st1": lambda e, a: st(e, 2, 3, slice(a, a + 1)),
-            "cast1": lambda e, a: cast(e, 2, 3, slice(a, a + 1)),
-            "ty1": lambda e, a: ty(e, 2, 3, slice(a, a + 1)),
-            "gy1": lambda e, a: gy(e, 2, 3, slice(a, a + 1)),
-            "qy1": lambda e, a: qy(e, 2, 6 + a, 1),
-        }
-        for step in ORDER:
-            steps[step[0]](*step[1:])
+        S, G, V = "scalar", "gpsimd", "vector"
+
+        order_b_codes(0)
+        order_b_scales(0)
+        order_b_scales(1)
+        turn_x(0)
+        turn_x(1)
+        quantize_x(0)
+        turn_x(2)
+        turn_x(3)
+        order_b_codes(1)
+        quantize_x(1)
+        lay(S, "r", 0, 0, 2)
+        lay(S, "r", 1, 0, 2)
+        noise(0, 0)
+
+        lay(G, "e", 0, 0, 1)
+        lay(S, "r", 0, 2, 2)
+        noise(0, 1)
+        quantize_pieces(("r", 0, 0), ("e", 0, 0))
+
+        lay(G, "e", 1, 0, 1)
+        lay(S, "r", 1, 2, 2)
+        noise(1, 0)
+        quantize_pieces(("r", 1, 0), ("r", 0, 2), ("e", 1, 0))
+
+        lay(G, "e", 0, 1, 1)
+        lay(S, "e", 1, 1, 1)
+        lay(S, "e", 0, 2, 2)
+        noise(1, 1)
+        quantize_pieces(("r", 1, 2), ("e", 0, 1))
+
+        lay(G, "c", 0, 0, 1)
+        lay(S, "e", 1, 2, 2)
+        lay(S, "c", 1, 0, 2)
+        counterfactual(0, 0, 1)
+        counterfactual(1, 0, 1)
+        quantize_pieces(("e", 1, 1), ("e", 0, 2))
+        quantize_z(0, 0, 1)
+        quantize_z(1, 0, 1)
+        counterfactual(0, 2, 3)
+        quantize_pieces(("e", 1, 2), ("c", 0, 0))
+
+        lay(G, "c", 0, 1, 1)
+        lay(S, "c", 1, 2, 2)
+        counterfactual(1, 2, 3)
+        counterfactual(0, 4, 5)
+        quantize_pieces(("c", 1, 0))
+        quantize_z(0, 1, 1)
+        quantize_z(1, 1, 1)
+        quantize_pieces(("c", 0, 1))
+
+        lay(G, "c", 0, 2, 1)
+        counterfactual(0, 6, 7)
+        outcomes(0, 0)
+        round_y(S, 0, 0)
+        quantize_z(0, 2, 2)
+        quantize_pieces(("c", 1, 2), ("c", 0, 2))
+
+        lay(G, "c", 0, 3, 1)
+        lay(S, "c", 1, 4, 2)
+        counterfactual(1, 4, 5)
+        outcomes(0, 1)
+        round_y(S, 0, 1)
+        quantize_pieces(("c", 0, 3))
+
+        lay(G, "c", 0, 4, 1)
+        counterfactual(1, 6, 7)
+        outcomes(1, 0)
+        round_y(S, 1, 0)
+        quantize_z(1, 2, 2)
+        quantize_pieces(("c", 0, 4))
+
+        lay(G, "c", 0, 5, 1)
+        blocks = [(oc, 2 * half + i) for oc, half in ((0, 0), (1, 0), (0, 1), (1, 1), (2, 0), (2, 1)) for i in range(2)]
+        for n in range(3, 11, 2):
+            outcomes(*blocks[n])
+            if n < 9:
+                round_y(S, *blocks[n])
+            outcomes(*blocks[n + 1])
+            turn_y(*blocks[n - 3])
+            turn_y(*blocks[n - 2])
+            if n == 9:
+                round_y(S, *blocks[n])
+            round_y(S if n == 3 else G if n < 9 else V, *blocks[n + 1])
+            if n == 3:
+                quantize_pieces(("c", 1, 4), ("c", 0, 5))
+            else:
+                finish_half(blocks[n - 5][0], blocks[n - 5][1] // 2)
+        finish_half(1, 1)
+        store_scales(slice(0, 2), [nc.sync])
+        for a in range(2):
+            outcome(2, 3, a)
+            store_y(2, 3, slice(a, a + 1))
+        turn_y(2, 0)
+        turn_y(2, 2)
+        turn_y(2, 1)
+        for a in range(2):
+            round_y(V, 2, 3, slice(a, a + 1))
+        for a in range(2):
+            turn_y(2, 3, slice(a, a + 1))
+        quantize_y(2, 4, 2)
+        store_words(2, 2, 1)
+        finish_half(2, 0)
+        quantize_y(2, 6, 1)
+        quantize_y(2, 7, 1)
+        store_words(2, 3, 1)
+        store_scales(slice(2, 3), [nc.sync, nc.scalar])

@@ -195,13 +195,12 @@ def tile_structural_model_counterfactual_k1_kernel(
             cols = span(first, count, QUARTER)
             piece = piece_tile(engine)[:, : count * QUARTER * SLOTS]
             if name == "r":
-                dst = piece.rearrange("p (s m t) -> p m s t", s=SLOTS, t=SLOTS)
-                src = r_raw[:, g, :, cols].rearrange("p t (m s) -> p m s t", s=SLOTS)
+                dst = piece.rearrange("p (s m i t) -> p m s i t", s=SLOTS, i=2, t=SLOTS)
+                src = r_raw[:, g, :, cols].rearrange("p t (m i s) -> p m s i t", i=2, s=SLOTS)
             else:
                 rows = e_t[:, g, :, cols] if name == "e" else c_raw[:, g, :, cols]
-                run = 1 if engine == "gpsimd" else 2 if name == "e" else 4
-                dst = piece.rearrange("p (n i t) -> p n t i", i=run, t=SLOTS)
-                src = rows.rearrange("p t (n i) -> p n t i", i=run)
+                dst = piece.rearrange("p (n t) -> p n t", t=SLOTS)
+                src = rows.rearrange("p t n -> p n t")
             move(engine, dst, src)
             staged[name, g, first] = (cols, piece)
 

from contextlib import ExitStack

import concourse.mybir as mybir
from concourse.masks import make_identity

UNITS, VARS, OUTS = 1024, 1024, 1536
FLOPS = 2 * UNITS * VARS * (2 * VARS + OUTS)

F32 = mybir.dt.float32
BF16 = mybir.dt.bfloat16
U32 = mybir.dt.uint32
I32 = mybir.dt.int32
U8 = mybir.dt.uint8
FP8X4 = mybir.dt.float8_e4m3fn_x4
FP4X4 = mybir.dt.float4_e2m1fn_x4
ADD = mybir.AluOpType.add
SUB = mybir.AluOpType.subtract
MULT = mybir.AluOpType.mult

P = 128
SLOTS = 4
GROUP = P * SLOTS
VAR_GROUPS = VARS // GROUP
OUT_GROUPS = OUTS // GROUP
QUARTER = 2 * P
HALF = 2 * QUARTER


def tile_structural_model_counterfactual_k1_kernel(
    tc, x, b_words, b_scales, shift, r, c, bias, out_0, out_1, out_2
):
    nc = tc.nc
    with ExitStack() as ctx:
        keep = ctx.enter_context(tc.tile_pool(name="keep", bufs=1))
        stage = ctx.enter_context(tc.tile_pool(name="stage", bufs=1))
        psum = ctx.enter_context(tc.psum_pool(name="psum", bufs=1))
        ctx.enter_context(tc.manual_schedule())

        def kept(name, shape, dtype):
            return keep.tile(shape, dtype, name=name, align_bytes=64)

        def planes(name, groups, width):
            return kept(name + "_codes", [P, groups, width], U32), kept(name + "_scales", [P, groups, width], U8)

        ident = kept("ident", [P, P], F32)
        b_raw = kept("b_raw", [P, VAR_GROUPS, VAR_GROUPS, 2 * GROUP], U8)
        b_codes = kept("b_codes", [P, VAR_GROUPS, 2 * VARS], U8)
        b_scales_raw = kept("b_scales_raw", [P, VAR_GROUPS, VARS], U8)
        b_scales_sb = kept("b_scales_sb", [P, VAR_GROUPS, VARS], U8)
        shift_sb = kept("shift_sb", [P, VAR_GROUPS, SLOTS], BF16)
        bias_sb = kept("bias_sb", [P, OUTS], BF16)
        r_raw = kept("r_raw", [P, VAR_GROUPS, SLOTS, VARS], BF16)
        c_raw = kept("c_raw", [P, VAR_GROUPS, SLOTS, OUTS], BF16)
        x_t = kept("x_t", [P, VAR_GROUPS, UNITS, SLOTS], BF16)
        e_t = kept("e_t", [P, VAR_GROUPS, SLOTS, UNITS], F32)
        mx = {
            "x": planes("x", VAR_GROUPS, UNITS),
            "e": planes("e", VAR_GROUPS, UNITS),
            "z": planes("z", VAR_GROUPS, UNITS),
            "r": planes("r", VAR_GROUPS, VARS),
            "c": planes("c", VAR_GROUPS, OUTS),
            "y": planes("y", OUT_GROUPS, UNITS),
        }

        def sum_bank():
            return psum.tile([P, GROUP], F32, name="sum_bank", bufs=5)

        def turn_bank():
            return psum.tile([P, 2, QUARTER], F32, name="turn_bank", bufs=3)

        def rows_tile(dtype, width):
            return stage.tile([P, 2, width], dtype, name="rows", bufs=4)

        def piece_tile(engine):
            if engine == "gpsimd":
                return stage.tile([P, QUARTER * SLOTS], BF16, name="gpsimd_piece", bufs=1, align_bytes=64)
            return stage.tile([P, HALF * SLOTS], BF16, name="piece", bufs=5, align_bytes=64)

        def span(first, count, width):
            return slice(first * width, (first + count) * width)

        nc.vector.memset(b_scales_raw[:].rearrange("p g n -> p (g n)").bitcast(I32), 0)
        make_identity(nc, ident[:])

        def load_b(go):
            nc.sync.dma_start(
                out=b_raw[:, go].bitcast(I32),
                in_=b_words[:, :, span(go, 1, 2 * GROUP)].rearrange("g p n -> p g n").bitcast(I32),
            )

        x_rows = x.rearrange("(i p) k -> p i k", p=P)
        x_raw = [rows_tile(BF16, VARS) for quarter in range(4)]
        load_b(0)
        nc.sync.dma_start(out=x_raw[0][:], in_=x_rows[:, 0:2, :])
        for q in range(4):
            nc.sync.dma_start(
                out=b_scales_raw[32 * q : 32 * q + 4, :, :].bitcast(I32),
                in_=b_scales[:, 4 * q : 4 * q + 4, :].rearrange("g j n -> j g n").bitcast(I32),
            )
        for a in range(2):
            nc.sync.dma_start(out=x_raw[1][:, a, :], in_=x_rows[:, 2 + a, :])
        nc.sync.dma_start(out=shift_sb[:], in_=shift.rearrange("(g p t) -> p g t", p=P, t=SLOTS))
        for quarter in range(2, 4):
            nc.sync.dma_start(out=x_raw[quarter][:], in_=x_rows[:, span(quarter, 1, 2), :])
        load_b(1)
        for raw, weight in ((r_raw, r), (c_raw, c)):
            for g in range(VAR_GROUPS):
                nc.sync.dma_start(
                    out=raw[:, g], in_=weight[span(g, 1, GROUP), :].rearrange("(p t) n -> p t n", t=SLOTS)
                )
        nc.sync.dma_start(out=bias_sb[:], in_=bias.partition_broadcast(P))

        staged = {}

        def move(engine, dst, src):
            if engine == "scalar":
                nc.scalar.copy(out=dst, in_=src)
            elif engine == "vector":
                nc.vector.tensor_copy(out=dst, in_=src)
            else:
                nc.gpsimd.tensor_scalar(out=dst, in0=src, scalar1=1.0, scalar2=0.0, op0=MULT, op1=ADD)

        def quantize(name, g, cols, values):
            codes, scales = mx[name]
            nc.vector.quantize_mx(out=codes[:, g, cols].bitcast(FP8X4), scales=scales[:, g, cols], in_=values)

        def operand(name, g, cols):
            if name == "b":
                return b_codes[:, g, 2 * cols.start : 2 * cols.stop].bitcast(FP4X4), b_scales_sb[:, g, cols]
            codes, scales = mx[name]
            return codes[:, g, cols].bitcast(FP8X4), scales[:, g, cols]

        def product(out, stationary, stationary_cols, moving, moving_cols):
            for g in range(VAR_GROUPS):
                lhs_codes, lhs_scales = operand(stationary, g, stationary_cols)
                rhs_codes, rhs_scales = operand(moving, g, moving_cols)
                nc.tensor.matmul_mx(
                    out=out,
                    lhsT=lhs_codes,
                    lhsT_scale=lhs_scales,
                    rhs=rhs_codes,
                    rhs_scale=rhs_scales,
                    start=(g == 0),
                    stop=(g == VAR_GROUPS - 1),
                )

        def order_b_codes(go):
            for g in range(VAR_GROUPS):
                nc.vector.tensor_copy(
                    out=b_codes[:, g, span(go, 1, 2 * GROUP)].rearrange("p (t m e) -> p t m e", t=SLOTS, e=2),
                    in_=b_raw[:, go, g, :].rearrange("p (m t e) -> p t m e", t=SLOTS, e=2),
                )

        def order_b_scales(go):
            cols = span(go, 1, GROUP)
            nc.vector.tensor_copy(
                out=b_scales_sb[:, :, cols].rearrange("p g (t m) -> p g t m", t=SLOTS),
                in_=b_scales_raw[:, :, cols].rearrange("p g (m t) -> p g t m", t=SLOTS),
            )

        def turn_x(quarter):
            for g in range(VAR_GROUPS):
                bank = turn_bank()
                for a in range(2):
                    words = x_raw[quarter][:, a, :].bitcast(F32)
                    for h in range(2):
                        nc.tensor.transpose(
                            bank[:, h, span(a, 1, P)], words[:, 256 * g + h : 256 * (g + 1) : 2], ident[:]
                        )
                nc.scalar.copy(
                    out=x_t[:].bitcast(F32)[:, g, span(quarter, 1, QUARTER), :],
                    in_=bank[:].rearrange("p h u -> p u h"),
                )

        def quantize_x(half):
            units = span(half, 1, HALF)
            for g in range(VAR_GROUPS):
                quantize("x", g, units, x_t[:, g, units, :].rearrange("p u t -> p (u t)"))

        def noise(half, go):
            units = span(half, 1, HALF)
            for t in range(SLOTS):
                bank = sum_bank()
                product(bank[:], "b", span(go * SLOTS + t, 1, P), "x", units)
                nc.vector.scalar_tensor_tensor(
                    out=e_t[:, go, t, units],
                    in0=x_t[:, go, units, t],
                    scalar=shift_sb[:, go, t : t + 1],
                    in1=bank[:],
                    op0=ADD,
                    op1=SUB,
                )

        def lay(engine, name, g, first, count):
            cols = span(first, count, QUARTER)
            piece = piece_tile(engine)[:, : count * QUARTER * SLOTS]
            if name == "r":
                dst = piece.rearrange("p (s m i t) -> p m s i t", s=SLOTS, i=2, t=SLOTS)
                src = r_raw[:, g, :, cols].rearrange("p t (m i s) -> p m s i t", i=2, s=SLOTS)
            else:
                rows = e_t[:, g, :, cols] if name == "e" else c_raw[:, g, :, cols]
                dst = piece.rearrange("p (n t) -> p n t", t=SLOTS)
                src = rows.rearrange("p t n -> p n t")
            move(engine, dst, src)
            staged[name, g, first] = (cols, piece)

        def quantize_pieces(*keys):
            for name, g, first in keys:
                quantize(name, g, *staged[name, g, first])

        def counterfactual(go, *tiles):
            for ut in tiles:
                units = span(ut, 1, P)
                half, a = divmod(ut, 4)
                bank = sum_bank()[:].rearrange("p (t u) -> p t u", t=SLOTS)
                for t in range(SLOTS):
                    product(bank[:, t, :], "r", span(go * SLOTS + t, 1, P), "e", units)
                if a == 0:
                    staged["z", go, half] = stage.tile([P, 4, GROUP], BF16, name="z_t", bufs=3, align_bytes=64)
                nc.vector.tensor_tensor(
                    out=staged["z", go, half][:, a, :].rearrange("p (u i t) -> p u t i", i=2, t=SLOTS),
                    in0=bank.rearrange("p t (u i) -> p u t i", i=2),
                    in1=e_t[:, go, :, units].rearrange("p t (u i) -> p u t i", i=2),
                    op=ADD,
                )

        def quantize_z(go, first, count):
            values = staged["z", go, first // 2][:, span(first % 2, count, 2), :]
            quantize("z", go, span(first, count, QUARTER), values.rearrange("p a n -> p (a n)"))

        BOTH = slice(0, 2)

        def outcome(oc, quarter, a):
            cols = span(oc, 1, GROUP)
            bank = sum_bank()
            product(bank[:], "z", span(2 * quarter + a, 1, P), "c", cols)
            if a == 0:
                staged["y", oc, quarter] = rows_tile(F32, GROUP)
            nc.vector.tensor_tensor(out=staged["y", oc, quarter][:, a, :], in0=bank[:], in1=bias_sb[:, cols], op=ADD)

        def store_y(oc, quarter, tiles):
            rows = out_0[span(quarter, 1, QUARTER), span(oc, 1, GROUP)].rearrange("(a p) o -> p a o", p=P)
            nc.sync.dma_start(out=rows[:, tiles, :], in_=staged["y", oc, quarter][:, tiles, :])

        def outcomes(oc, quarter):
            for a in range(2):
                outcome(oc, quarter, a)
            store_y(oc, quarter, BOTH)

        def round_y(engine, oc, quarter, tiles=BOTH):
            if tiles.start == 0:
                staged["y16", oc, quarter] = stage.tile([P, 2, QUARTER, 2], BF16, name="y16", bufs=5)
            cols = slice(tiles.start * P, tiles.stop * P)
            src = staged["y", oc, quarter][:].rearrange("p a (m h e) -> p h (a m) e", h=2, e=2)
            move(engine, staged["y16", oc, quarter][:, :, cols, :], src[:, :, cols, :])

        def turn_y(oc, quarter, tiles=BOTH):
            words = staged["y16", oc, quarter][:].rearrange("p h n e -> p h (n e)").bitcast(F32)
            bank = turn_bank()
            for a in range(tiles.start, tiles.stop):
                for h in range(2):
                    nc.tensor.transpose(bank[:, h, span(a, 1, P)], words[:, h, span(a, 1, P)], ident[:])
            if quarter % 2 == 0:
                staged["y_t", oc, quarter // 2] = piece_tile("scalar")
            units = slice(tiles.start * P, tiles.stop * P)
            part = staged["y_t", oc, quarter // 2][:, span(quarter % 2, 1, QUARTER * SLOTS)]
            nc.scalar.copy(
                out=part.bitcast(F32).rearrange("p (u h) -> p u h", h=2)[:, units, :],
                in_=bank[:].rearrange("p h u -> p u h")[:, units, :],
            )

        def quantize_y(oc, first, count):
            quantize("y", oc, span(first, count, P), staged["y_t", oc, first // 4][:, span(first % 4, count, GROUP)])

        def store_words(oc, first, count):
            units = span(first, count, QUARTER)
            nc.sync.dma_start(
                out=out_1[oc].rearrange("p m t -> p (m t)").bitcast(I32)[:, units],
                in_=mx["y"][0][:, oc, units].bitcast(I32),
            )

        def finish_half(oc, half):
            quantize_y(oc, 4 * half, 4)
            store_words(oc, 2 * half, 2)

        def store_scales(groups, queues):
            for q in range(4):
                queues[q % len(queues)].dma_start(
                    out=out_2[groups, 4 * q : 4 * q + 4, :].rearrange("g j n -> j g n").bitcast(I32),
                    in_=mx["y"][1][32 * q : 32 * q + 4, groups, :].bitcast(I32),
                )

        S, G, V = "scalar", "gpsimd", "vector"

        order_b_codes(0)
        order_b_scales(0)
        order_b_scales(1)
        turn_x(0)
        turn_x(1)
        quantize_x(0)
        turn_x(2)
        turn_x(3)
        order_b_codes(1)
        quantize_x(1)
        lay(S, "r", 0, 0, 2)
        lay(S, "r", 1, 0, 2)
        noise(0, 0)

        lay(G, "e", 0, 0, 1)
        lay(S, "r", 0, 2, 2)
        noise(0, 1)
        quantize_pieces(("r", 0, 0), ("e", 0, 0))

        lay(G, "e", 1, 0, 1)
        lay(S, "r", 1, 2, 2)
        noise(1, 0)
        quantize_pieces(("r", 1, 0), ("r", 0, 2), ("e", 1, 0))

        lay(G, "e", 0, 1, 1)
        lay(S, "e", 1, 1, 1)
        lay(S, "e", 0, 2, 2)
        noise(1, 1)
        quantize_pieces(("r", 1, 2), ("e", 0, 1))

        lay(G, "c", 0, 0, 1)
        lay(S, "e", 1, 2, 2)
        lay(S, "c", 1, 0, 2)
        counterfactual(0, 0, 1)
        counterfactual(1, 0, 1)
        quantize_pieces(("e", 1, 1), ("e", 0, 2))
        quantize_z(0, 0, 1)
        quantize_z(1, 0, 1)
        counterfactual(0, 2, 3)
        quantize_pieces(("e", 1, 2), ("c", 0, 0))

        lay(G, "c", 0, 1, 1)
        lay(S, "c", 1, 2, 2)
        counterfactual(1, 2, 3)
        counterfactual(0, 4, 5)
        quantize_pieces(("c", 1, 0))
        quantize_z(0, 1, 1)
        quantize_z(1, 1, 1)
        quantize_pieces(("c", 0, 1))

        lay(G, "c", 0, 2, 1)
        counterfactual(0, 6, 7)
        outcomes(0, 0)
        round_y(S, 0, 0)
        quantize_z(0, 2, 2)
        quantize_pieces(("c", 1, 2), ("c", 0, 2))

        lay(G, "c", 0, 3, 1)
        lay(S, "c", 1, 4, 2)
        counterfactual(1, 4, 5)
        outcomes(0, 1)
        round_y(S, 0, 1)
        quantize_pieces(("c", 0, 3))

        lay(G, "c", 0, 4, 1)
        counterfactual(1, 6, 7)
        outcomes(1, 0)
        round_y(S, 1, 0)
        quantize_z(1, 2, 2)
        quantize_pieces(("c", 0, 4))

        lay(G, "c", 0, 5, 1)
        blocks = [(oc, 2 * half + i) for oc, half in ((0, 0), (1, 0), (0, 1), (1, 1), (2, 0), (2, 1)) for i in range(2)]
        for n in range(3, 11, 2):
            outcomes(*blocks[n])
            if n < 9:
                round_y(S, *blocks[n])
            outcomes(*blocks[n + 1])
            turn_y(*blocks[n - 3])
            turn_y(*blocks[n - 2])
            if n == 9:
                round_y(S, *blocks[n])
            round_y(S if n == 3 else G if n < 9 else V, *blocks[n + 1])
            if n == 3:
                quantize_pieces(("c", 1, 4), ("c", 0, 5))
            else:
                finish_half(blocks[n - 5][0], blocks[n - 5][1] // 2)
        finish_half(1, 1)
        store_scales(slice(0, 2), [nc.sync])
        for a in range(2):
            outcome(2, 3, a)
            store_y(2, 3, slice(a, a + 1))
        turn_y(2, 0)
        turn_y(2, 2)
        turn_y(2, 1)
        for a in range(2):
            round_y(V, 2, 3, slice(a, a + 1))
        for a in range(2):
            turn_y(2, 3, slice(a, a + 1))
        quantize_y(2, 4, 2)
        store_words(2, 2, 1)
        finish_half(2, 0)
        quantize_y(2, 6, 1)
        quantize_y(2, 7, 1)
        store_words(2, 3, 1)
        store_scales(slice(2, 3), [nc.sync, nc.scalar])
